import numpy as np
import ml_dtypes


def mxq(x, axis, fmt="e4m3"):
    dtype, down = {"e4m3": (ml_dtypes.float8_e4m3fn, 7), "e5m2": (ml_dtypes.float8_e5m2, 14)}[fmt]
    v = np.moveaxis(np.asarray(x, np.float32).astype(ml_dtypes.bfloat16).astype(np.float64), axis, -1)
    blocks = v.reshape(v.shape[:-1] + (-1, 32))
    amax = np.abs(blocks).max(-1, keepdims=True)
    byte = np.maximum(np.where(amax > 0, np.frexp(amax)[1] - 1 + 127, 0) - down, 1)
    scale = np.exp2(byte - 127.0)
    codes = (blocks / scale).astype(np.float32).astype(dtype).astype(np.float64)
    return np.moveaxis((codes * scale).reshape(v.shape), -1, axis)


WIDE = False


def mx_kscale(k):
    if not WIDE:
        return np.ones(k)
    levels = np.array([10, -10, 5, -5, 0])
    if k % 512:
        return np.exp2(np.random.permutation(np.resize(levels, k // 32))).repeat(32)
    a = np.empty((k // 512, 16))
    for p in range(k // 512):
        a[p, :8] = np.random.permutation(np.resize(levels, 8))
        for g in range(8):
            far = levels[np.abs(levels - a[p, g]) >= 10]
            a[p, g + 8] = far[np.random.randint(len(far))]
    return np.exp2(a.ravel()).repeat(32)


def f64(x):
    return np.asarray(x).astype(np.float64)


def striped(idx):
    return np.tile(idx.reshape(-1, 16).T, (8, 1)).astype(np.uint16)


def unstriped(offs):
    return offs[:16].T.reshape(-1).astype(np.int64)


E2M1 = np.array([0.0, 0.5, 1.0, 1.5, 2.0, 3.0, 4.0, 6.0, -0.0, -0.5, -1.0, -1.5, -2.0, -3.0, -4.0, -6.0])


def pack_weight(w, fmt):
    k, n = w.shape
    w = f64(np.asarray(w, np.float32).astype(ml_dtypes.bfloat16)).reshape(k // 32, 32, n)
    amax = np.abs(w).max(1)
    if fmt == "e4m3":
        byte = np.frexp(amax)[1] - 1 + 127 - 7
    else:
        mant, ex = np.frexp(amax / 6.0)
        byte = np.where(mant > 0.5, ex, ex - 1) + 127
    byte = np.clip(np.where(amax > 0, byte, 1), 1, 254)
    scaled = (w * np.exp2(127.0 - byte)[:, None, :]).reshape(k, n).astype(np.float32)
    by_word = np.ascontiguousarray(scaled.reshape(k // 512, 128, 4, n).transpose(0, 1, 3, 2))
    if fmt == "e4m3":
        words = by_word.astype(ml_dtypes.float8_e4m3fn).view(np.uint8)
    else:
        c = by_word.astype(ml_dtypes.float4_e2m1fn).view(np.uint8) & 0xF
        words = (c[..., 0::2] | (c[..., 1::2] << 4)).reshape(k // 512, 128, 2 * n)
    return np.ascontiguousarray(words), np.ascontiguousarray(byte.astype(np.uint8).reshape(k // 512, 16, n))


def unpack_weight(words, scales, fmt):
    g, _, n = scales.shape
    words = np.ascontiguousarray(words).reshape(g, 128, n, -1)
    if fmt == "e4m3":
        vals = words.view(ml_dtypes.float8_e4m3fn).astype(np.float64)
    else:
        nib = np.empty((g, 128, n, 4), np.uint8)
        nib[..., 0::2] = words & 0xF
        nib[..., 1::2] = words >> 4
        vals = E2M1[nib]
    vals = vals * np.repeat(np.exp2(scales.astype(np.float64) - 127.0), 8, axis=1)[..., None]
    return vals.transpose(0, 1, 3, 2).reshape(g * 512, n)


def gelu(v):
    return 0.5 * v * (1.0 + np.tanh(np.sqrt(2.0 / np.pi) * (v + 0.044715 * v**3)))


def bf(x):
    return np.asarray(x, np.float32).astype(ml_dtypes.bfloat16)


def planes(Y):
    n, m = Y.shape
    b = f64(bf(Y)).reshape(n // 32, 32, m)
    amax = np.abs(b).max(1)
    byte = np.clip(np.where(amax > 0, np.frexp(amax)[1] - 1 + 127 - 7, 1), 1, 254)
    codes = (b * np.exp2(127.0 - byte)[:, None, :]).reshape(n, m).astype(np.float32).astype(ml_dtypes.float8_e4m3fn).view(np.uint8)
    words = codes.reshape(n // 512, 128, 4, m).transpose(0, 1, 3, 2)
    return np.ascontiguousarray(words), np.ascontiguousarray(byte.astype(np.uint8).reshape(n // 512, 16, m))


K, T, S, R, R2, H, T2, P = 1024, 4096, 1024, 512, 1024, 1024, 2048, 1024


def setup_inputs():
    n = np.random.standard_normal
    s = mx_kscale(K)[:, None]
    q = mx_kscale(R2)[:, None]
    u = mx_kscale(H)[:, None]
    size = np.exp(0.8 * n(H))
    d = {}
    d["tab_words"], d["tab_scales"] = pack_weight(n((K, T)) * s, "e4m3")
    d["offs"] = striped(np.random.permutation(T)[:S])
    d["w1"] = (0.55 * n((K, R)) / K**0.5 / s).astype(np.float32)
    d["gsc"] = (np.exp(0.3 * n(R2)) * q[:, 0]).astype(np.float32)
    d["ws_words"], d["ws_scales"] = pack_weight(2.6 * n((R, H)) / R**0.5 / q[:R] * u.T, "e2m1")
    d["wc"] = (1.5 * n((R, H)) / R**0.5 / q[R:] * u.T).astype(np.float32)
    d["page0"] = (n((H, T2)) * u).astype(np.float32)
    d["wgs"] = np.exp(0.3 * n((128, S))).astype(np.float32)
    d["offs2"] = striped(np.random.permutation(T2)[:S])
    d["offs3"] = striped(np.random.permutation(T2)[:P])
    d["gx"] = np.exp(0.4 * n(H)).astype(np.float32)
    d["w2_words"], d["w2_scales"] = pack_weight(0.7 * n((H, H)) / H**0.5 / u * size[None, :], "e4m3")
    d["offs4"] = striped(np.random.permutation(T2)[:P])
    d["gn"] = (0.8 * np.exp(0.3 * n(H)) * size / u[:, 0]).astype(np.float32)
    return d


def reference(tab_words, tab_scales, offs, w1, gsc, ws_words, ws_scales, wc, page0, wgs, offs2, offs3, gx, w2_words, w2_scales, offs4, gn):
    v = unpack_weight(tab_words, tab_scales, "e4m3")[:, unstriped(offs)]
    ph = mxq(f64(w1), 0, "e4m3").T @ v
    sc = mxq(np.vstack([np.sin(ph), np.cos(ph)]) * f64(gsc)[:, None], 0, "e4m3")
    hs = unpack_weight(ws_words, ws_scales, "e2m1").T @ sc[:R]
    hc = mxq(f64(wc), 0, "e4m3").T @ sc[R:]
    h = np.maximum(hs, hc)
    page = f64(page0).copy()
    page[:, unstriped(offs2)] = np.tile(f64(wgs), (H // 128, 1)) * h
    x = mxq(page[:, unstriped(offs3)] * f64(gx)[:, None], 0, "e4m3")
    enc = unpack_weight(w2_words, w2_scales, "e4m3").T @ x
    y = enc + page[:, unstriped(offs4)] * f64(gn)[:, None]
    words, scales = planes(y)
    return y, words, scales

@@ -1,0 +1,373 @@
+import math
+from contextlib import ExitStack
+
+import concourse.mybir as mybir
+
+F32 = mybir.dt.float32
+BF16 = mybir.dt.bfloat16
+I32 = mybir.dt.int32
+U32 = mybir.dt.uint32
+U16 = mybir.dt.uint16
+U8 = mybir.dt.uint8
+FP8X4 = mybir.dt.float8_e4m3fn_x4
+FP4X4 = mybir.dt.float4_e2m1fn_x4
+ALU = mybir.AluOpType
+ACT = mybir.ActivationFunctionType
+
+P = 128
+K, T, S, R, H, T2 = 1024, 4096, 1024, 512, 1024, 2048
+FLOPS = 2 * (K * R * S + 2 * R * H * S + H * H * S)
+
+CHUNK = 256
+CHUNKS = S // CHUNK
+HALF = S // 2
+TWO_PI = 2.0 * math.pi
+ROUNDER = 1.5 * 2.0**23
+
+
+def deal_and_round(copy, grouped, raw, first, count):
+    dst = grouped[:].rearrange("p (t mm m2 j) -> p mm j m2 t", t=4, m2=2, j=4)[:, first : first + count]
+    copy(out=dst, in_=raw[:].rearrange("p j (mm m2 t) -> p mm j m2 t", m2=2, t=4))
+
+
+def interleave(copy, grouped, planes):
+    copy(
+        out=grouped.rearrange("p (c i t) -> p c t i", i=4, t=4),
+        in_=planes.rearrange("p t (c i) -> p c t i", i=4),
+    )
+
+
+def tile_list_blade_tip_page_kernel(
+    tc, tab_words, tab_scales, offs, w1, gsc, ws_words, ws_scales, wc, page0, wgs, offs2, offs3, gx,
+    w2_words, w2_scales, offs4, gn, out_0, out_1, out_2,
+):
+    nc = tc.nc
+
+    with ExitStack() as ctx:
+        keep = ctx.enter_context(tc.tile_pool(name="keep", bufs=1))
+        psum = ctx.enter_context(tc.psum_pool(name="psum", bufs=1))
+
+        list1 = keep.tile([P, S // 16], U16, name="list1")
+        list2 = keep.tile([P, S // 16], U16, name="list2")
+        list3 = keep.tile([P, S // 16], U16, name="list3")
+        list4 = keep.tile([P, S // 16], U16, name="list4")
+        gsc_sb = keep.tile([P, 2, 4], F32, name="gsc_sb")
+        gx_sb = keep.tile([P, 2, 4], F32, name="gx_sb")
+        gn_sb = keep.tile([P, 2, 4], F32, name="gn_sb")
+        pages = [keep.tile([P, T2], F32, name="page%d" % i) for i in range(8)]
+        wgs_first = keep.tile([P, 4, CHUNK], F32, name="wgs_first")
+        wgs_rest = keep.tile([P, 4, S - CHUNK], F32, name="wgs_rest")
+        f_codes = [keep.tile([P, S], U32, name="f_codes%d" % h, align_bytes=64) for h in range(2)]
+        f_scales = [keep.tile([P, S], U8, name="f_scales%d" % h, align_bytes=64) for h in range(2)]
+        wc_codes = [keep.tile([P, 512], U32, name="wc_codes%d" % b, align_bytes=64) for b in range(2)]
+        wc_scales = [keep.tile([P, 512], U8, name="wc_scales%d" % b, align_bytes=64) for b in range(2)]
+        ws_dealt = keep.tile([P, 2 * H], U8, name="ws_dealt", align_bytes=64)
+        wscale_dealt = keep.tile([P, H], U8, name="wscale_dealt", align_bytes=64)
+
+        page_rows = page0.rearrange("(b p t) c -> b t p c", b=2, t=4)
+        wgs_rows = wgs.rearrange("(q t) j -> q t j", t=4)
+        wc_rows = wc.rearrange("(p j) c -> p j c", j=4)
+
+        hs_tiles = {}
+
+        def first_products(c):
+            cols = slice(c * CHUNK, (c + 1) * CHUNK)
+            for pair in range(4):
+                bank = psum.tile([P, 2, CHUNK], F32, name="hs_bank", tag="hs_bank", bufs=2)
+                for e in range(2):
+                    i = 2 * pair + e
+                    nc.tensor.matmul_mx(
+                        out=bank[:, e, :],
+                        lhsT=ws_dealt[:, 256 * i : 256 * (i + 1)].bitcast(FP4X4),
+                        lhsT_scale=wscale_dealt[:, P * i : P * (i + 1)],
+                        rhs=f_codes[0][:, cols].bitcast(FP8X4),
+                        rhs_scale=f_scales[0][:, cols],
+                        start=True, stop=True,
+                    )
+                hs = keep.tile([P, 2, CHUNK], F32, name="hs", tag="hs", bufs=4)
+                nc.scalar.copy(out=hs[:], in_=bank[:])
+                hs_tiles[c, pair] = hs
+
+        def place_pair(c, pair):
+            cols = slice(c * CHUNK, (c + 1) * CHUNK)
+            bank = psum.tile([P, 2, CHUNK], F32, name="hc_bank", tag="hc_bank", bufs=3)
+            for e in range(2):
+                b, t = divmod(2 * pair + e, 4)
+                nc.tensor.matmul_mx(
+                    out=bank[:, e, :],
+                    lhsT=wc_codes[b][:, P * t : P * (t + 1)].bitcast(FP8X4),
+                    lhsT_scale=wc_scales[b][:, P * t : P * (t + 1)],
+                    rhs=f_codes[1][:, cols].bitcast(FP8X4),
+                    rhs_scale=f_scales[1][:, cols],
+                    start=True, stop=True,
+                )
+            h = keep.tile([P, 2, CHUNK], F32, name="h", tag="h", bufs=2)
+            nc.vector.tensor_tensor(out=h[:], in0=bank[:], in1=hs_tiles[c, pair][:], op=ALU.max)
+            for e in range(2):
+                i = 2 * pair + e
+                t = i % 4
+                weight = wgs_first[:, t, :] if c == 0 else wgs_rest[:, t, (c - 1) * CHUNK : c * CHUNK]
+                places = list2[:, c * CHUNK // 16 : (c + 1) * CHUNK // 16]
+                nc.vector.tensor_tensor(pages[i][:].indirect(places), h[:, e, :], weight, ALU.mult)
+
+        with tc.tile_pool(name="early", bufs=1) as early:
+            tab_sb = [early.tile([P, T], U32, name="tab_sb%d" % a) for a in range(2)]
+            tab_scale_sb = early.tile([P, T], U8, name="tab_scale_sb")
+            wscale_raw = early.tile([P, H], U8, name="wscale_raw")
+            ws_raw = early.tile([P, 2 * H], U8, name="ws_raw")
+            v_codes = [early.tile([P, S], U32, name="v_codes%d" % a, align_bytes=64) for a in range(2)]
+            v_scales = early.tile([P, S], U8, name="v_scales", align_bytes=64)
+            w1_codes = [early.tile([P, R], U32, name="w1_codes%d" % a, align_bytes=64) for a in range(2)]
+            w1_scales = [early.tile([P, R], U8, name="w1_scales%d" % a, align_bytes=64) for a in range(2)]
+            w1_raw0 = early.tile([P, 4, R], F32, name="w1_raw0", tag="raw_a")
+            w1_raw1 = [early.tile([P, 4, R // 2], F32, name="w1_raw1_%d" % u) for u in range(2)]
+            wc_raw0 = early.tile([P, 4, 512], F32, name="wc_raw0")
+
+            nc.vector.memset(tab_scale_sb[:].bitcast(I32), 0)
+            nc.gpsimd.memset(wscale_raw[:].bitcast(I32), 0)
+            w1_rows = w1.rearrange("(a p j) c -> a p j c", a=2, j=4)
+            nc.sync.dma_start(list1[:], offs)
+            nc.sync.dma_start(out=gsc_sb[:], in_=gsc.rearrange("(h p t) -> p h t", h=2, t=4))
+            nc.sync.dma_start(list2[:], offs2)
+            nc.sync.dma_start(list3[:], offs3)
+            nc.sync.dma_start(list4[:], offs4)
+            nc.sync.dma_start(out=ws_raw[:].bitcast(I32), in_=ws_words[0].bitcast(I32))
+            for a in range(2):
+                nc.sync.dma_start(
+                    out=tab_sb[a][:].bitcast(I32), in_=tab_words[a].rearrange("p t i -> p (t i)").bitcast(I32)
+                )
+            for q in range(4):
+                nc.scalar.dma_start(
+                    out=tab_scale_sb[32 * q : 32 * q + 8, :].bitcast(I32),
+                    in_=tab_scales[:, 4 * q : 4 * q + 4, :].bitcast(I32),
+                )
+            for q in range(4):
+                nc.scalar.dma_start(
+                    out=wscale_raw[32 * q : 32 * q + 4, :].bitcast(I32),
+                    in_=ws_scales[0, 4 * q : 4 * q + 4, :].bitcast(I32),
+                )
+            for q in range(4):
+                nc.gpsimd.dma_start(
+                    out=wscale_raw[32 * q + 4 : 32 * q + 12, :].bitcast(I32),
+                    in_=w2_scales[:, 4 * q : 4 * q + 4, :].bitcast(I32),
+                )
+            nc.sync.dma_start(out=w1_raw0[:], in_=w1_rows[0])
+            for u in range(2):
+                nc.sync.dma_start(out=w1_raw1[u][:], in_=w1_rows[1][:, :, u * 256 : (u + 1) * 256])
+            nc.sync.dma_start(out=wc_raw0[:], in_=wc_rows[:, :, 0:512])
+            nc.sync.dma_start(out=pages[0][:], in_=page_rows[0, 0])
+            for q in range(4):
+                nc.sync.dma_start(out=wgs_first[32 * q : 32 * (q + 1)], in_=wgs_rows[:, :, 0:CHUNK])
+            for i in range(1, 3):
+                nc.sync.dma_start(out=pages[i][:], in_=page_rows[i // 4, i % 4])
+
+            nc.vector.tensor_copy(v_codes[0][:], tab_sb[0][:].indirect(list1[:]))
+            nc.vector.tensor_copy(v_scales[:], tab_scale_sb[:].indirect(list1[:]))
+            nc.vector.tensor_copy(v_codes[1][:], tab_sb[1][:].indirect(list1[:]))
+
+            w1_grouped = [
+                early.tile([P, 4 * R], BF16, name="w1_grouped%d" % a, tag="w_grouped", bufs=2, align_bytes=64)
+                for a in range(2)
+            ]
+            deal_and_round(nc.scalar.copy, w1_grouped[0], w1_raw0, 0, 64)
+            nc.vector.tensor_copy(
+                out=ws_dealt[:].rearrange("p (b t m e) -> p b m t e", b=2, t=4, e=2),
+                in_=ws_raw[:].rearrange("p (b m t e) -> p b m t e", b=2, t=4, e=2),
+            )
+            nc.vector.tensor_copy(
+                out=wscale_dealt[:].rearrange("p (b t m) -> p b m t", b=2, t=4),
+                in_=wscale_raw[:].rearrange("p (b m t) -> p b m t", b=2, t=4),
+            )
+            for u in range(2):
+                deal_and_round(nc.vector.tensor_copy, w1_grouped[1], w1_raw1[u], 32 * u, 32)
+            for a in range(2):
+                nc.vector.quantize_mx(out=w1_codes[a][:].bitcast(FP8X4), scales=w1_scales[a][:], in_=w1_grouped[a][:])
+
+            wc_raw1 = early.tile([P, 4, 512], F32, name="wc_raw1", tag="raw_a")
+            nc.sync.dma_start(out=wc_raw1[:], in_=wc_rows[:, :, 512:1024])
+            for i in range(3, 8):
+                nc.sync.dma_start(out=pages[i][:], in_=page_rows[i // 4, i % 4])
+            for q in range(4):
+                nc.sync.dma_start(out=wgs_rest[32 * q : 32 * (q + 1)], in_=wgs_rows[:, :, CHUNK:S])
+            nc.sync.dma_start(out=gx_sb[:], in_=gx.rearrange("(b p t) -> p b t", b=2, t=4))
+            nc.sync.dma_start(out=gn_sb[:], in_=gn.rearrange("(b p t) -> p b t", b=2, t=4))
+
+            def phases(out, t, cols):
+                for a in range(2):
+                    nc.tensor.matmul_mx(
+                        out=out,
+                        lhsT=w1_codes[a][:, P * t : P * (t + 1)].bitcast(FP8X4),
+                        lhsT_scale=w1_scales[a][:, P * t : P * (t + 1)],
+                        rhs=v_codes[a][:, cols].bitcast(FP8X4),
+                        rhs_scale=v_scales[4 * a : P, cols],
+                        start=(a == 0), stop=(a == 1),
+                    )
+
+            def scratch(name, dtype, bufs):
+                return early.tile([P, 4 * CHUNK], dtype, name=name, tag=name, bufs=bufs, align_bytes=64)
+
+            def sine_and_cosine(sine, size, cosine, frac):
+                nc.scalar.activation(out=sine, in_=frac, func=ACT.Sin, scale=-TWO_PI)
+                nc.scalar.activation(out=size, in_=frac, func=ACT.Abs)
+                nc.scalar.activation(out=cosine, in_=size, func=ACT.Sin, scale=-TWO_PI, bias=math.pi / 2)
+
+            def quantize_wc(b, copy, raw):
+                grouped = early.tile([P, 4 * 512], BF16, name="wc_grouped", tag="w_grouped", bufs=2, align_bytes=64)
+                deal_and_round(copy, grouped, raw, 0, 64)
+                nc.vector.quantize_mx(out=wc_codes[b][:].bitcast(FP8X4), scales=wc_scales[b][:], in_=grouped[:])
+
+            turns, whole, frac = scratch("turns", F32, 1), scratch("whole", I32, 1), scratch("frac", F32, 2)
+            sine, size, cosine = scratch("sine", F32, 1), scratch("size", F32, 1), scratch("cosine", F32, 1)
+            grouped0 = [scratch("f_grouped%d" % h, BF16, 2) for h in range(2)]
+            for u in range(2):
+                bank = psum.tile([P, 4, P], F32, name="ph_bank0", tag="ph_bank", bufs=3)
+                for t in range(4):
+                    phases(bank[:, t, :], t, slice(u * P, (u + 1) * P))
+                part = slice(u * 4 * P, (u + 1) * 4 * P)
+                nc.scalar.activation(
+                    out=turns[:, part].rearrange("p (n t) -> p n t", t=4), in_=bank[:].rearrange("p t n -> p n t"),
+                    func=ACT.Copy, scale=1.0 / TWO_PI,
+                )
+                nc.vector.tensor_scalar(out=whole[:, part], in0=turns[:, part], scalar1=ROUNDER, scalar2=None, op0=ALU.add)
+                nc.vector.scalar_tensor_tensor(
+                    out=frac[:, part], in0=whole[:, part], scalar=ROUNDER, in1=turns[:, part],
+                    op0=ALU.subtract, op1=ALU.subtract,
+                )
+                sine_and_cosine(sine[:, part], size[:, part], cosine[:, part], frac[:, part])
+            quantize_wc(0, nc.vector.tensor_copy, wc_raw0)
+            for u in range(2):
+                part = slice(u * 4 * P, (u + 1) * 4 * P)
+                for h, values in enumerate((sine, cosine)):
+                    nc.vector.tensor_tensor(
+                        out=grouped0[h][:, part].rearrange("p (n t) -> p n t", t=4),
+                        in0=values[:, part].rearrange("p (n t) -> p n t", t=4),
+                        in1=gsc_sb[:, h : h + 1, :].to_broadcast([P, P, 4]),
+                        op=ALU.mult,
+                    )
+            for h in range(2):
+                nc.vector.quantize_mx(
+                    out=f_codes[h][:, 0:CHUNK].bitcast(FP8X4), scales=f_scales[h][:, 0:CHUNK], in_=grouped0[h][:]
+                )
+
+            fracs = {}
+
+            def reduce_phases(c):
+                turns, whole, frac = scratch("turns", F32, 1), scratch("whole", I32, 1), scratch("frac", F32, 2)
+                for u in range(2):
+                    bank = psum.tile([P, 2, CHUNK], F32, name="ph_bank", tag="ph_bank", bufs=3)
+                    for e in range(2):
+                        phases(bank[:, e, :], 2 * u + e, slice(c * CHUNK, (c + 1) * CHUNK))
+                    nc.scalar.activation(
+                        out=turns[:, u * 2 * CHUNK : (u + 1) * 2 * CHUNK], in_=bank[:].rearrange("p e n -> p (e n)"),
+                        func=ACT.Copy, scale=1.0 / TWO_PI,
+                    )
+                nc.scalar.activation(out=whole[:].bitcast(U32), in_=turns[:], func=ACT.Copy, bias=ROUNDER)
+                nc.vector.scalar_tensor_tensor(
+                    out=frac[:], in0=whole[:], scalar=ROUNDER, in1=turns[:], op0=ALU.subtract, op1=ALU.subtract
+                )
+                fracs[c] = frac
+
+            def features(c):
+                sine, size, cosine = scratch("sine", F32, 1), scratch("size", F32, 1), scratch("cosine", F32, 1)
+                sine_and_cosine(sine[:], size[:], cosine[:], fracs[c][:])
+                result = []
+                for h, values in enumerate((sine, cosine)):
+                    planes = early.tile([P, 4, CHUNK], BF16, name="f_planes%d" % h, tag="f_planes%d" % h)
+                    for t in range(4):
+                        nc.scalar.activation(
+                            out=planes[:, t, :], in_=values[:, t * CHUNK : (t + 1) * CHUNK], func=ACT.Copy,
+                            scale=gsc_sb[:, h, t : t + 1],
+                        )
+                    grouped = scratch("f_grouped%d" % h, BF16, 2)
+                    interleave(nc.scalar.copy, grouped[:], planes[:])
+                    result.append(grouped)
+                return result
+
+            def quantize_features(c, grouped):
+                cols = slice(c * CHUNK, (c + 1) * CHUNK)
+                for h in range(2):
+                    nc.vector.quantize_mx(
+                        out=f_codes[h][:, cols].bitcast(FP8X4), scales=f_scales[h][:, cols], in_=grouped[h][:]
+                    )
+
+            first_products(0)
+            reduce_phases(1)
+            for c in range(CHUNKS - 1):
+                place_pair(c, 0)
+                if c == 0:
+                    quantize_wc(1, nc.scalar.copy, wc_raw1)
+                grouped = features(c + 1)
+                place_pair(c, 1)
+                place_pair(c, 2)
+                quantize_features(c + 1, grouped)
+                first_products(c + 1)
+                if c + 2 < CHUNKS:
+                    reduce_phases(c + 2)
+                place_pair(c, 3)
+
+        with tc.tile_pool(name="late", bufs=1) as late:
+            w2_raw = [late.tile([P, H], U32, name="w2_raw%d" % a) for a in range(2)]
+            w2_dealt = [late.tile([P, H], U32, name="w2_dealt%d" % a, align_bytes=64) for a in range(2)]
+            x_codes = [late.tile([P, S], U32, name="x_codes%d" % b, align_bytes=64) for b in range(2)]
+            x_scales = [late.tile([P, S], U8, name="x_scales%d" % b, align_bytes=64) for b in range(2)]
+            y_codes = [late.tile([P, S], U32, name="y_codes%d" % g, align_bytes=64) for g in range(2)]
+            y_scales = late.tile([P, S], U8, name="y_scales", align_bytes=64)
+            for a in range(2):
+                nc.sync.dma_start(
+                    out=w2_raw[a][:].bitcast(I32), in_=w2_words[a].rearrange("p c i -> p (c i)").bitcast(I32)
+                )
+
+            for b in range(2):
+                place_pair(CHUNKS - 1, 2 * b)
+                place_pair(CHUNKS - 1, 2 * b + 1)
+                nc.vector.tensor_copy(
+                    out=w2_dealt[b][:].rearrange("p (g t m) -> p g m t", g=2, t=4),
+                    in_=w2_raw[b][:].rearrange("p (g m t) -> p g m t", g=2, t=4),
+                )
+                for u in range(2):
+                    cols = slice(u * HALF, (u + 1) * HALF)
+                    planes = late.tile([P, 4, HALF], BF16, name="x_planes", tag="x_planes", bufs=2)
+                    for t in range(4):
+                        picked = late.tile([P, HALF], F32, name="picked3", tag="picked3", bufs=4)
+                        nc.vector.tensor_copy(
+                            picked[:], pages[4 * b + t][:].indirect(list3[:, u * HALF // 16 : (u + 1) * HALF // 16])
+                        )
+                        nc.scalar.activation(out=planes[:, t, :], in_=picked[:], func=ACT.Copy, scale=gx_sb[:, b, t : t + 1])
+                    grouped = late.tile([P, 4 * HALF], BF16, name="x_grouped", tag="x_grouped", bufs=2, align_bytes=64)
+                    interleave(nc.scalar.copy, grouped[:], planes[:])
+                    nc.vector.quantize_mx(out=x_codes[b][:, cols].bitcast(FP8X4), scales=x_scales[b][:, cols], in_=grouped[:])
+
+            y_rows = out_0.rearrange("(g p t) j -> g p t j", g=2, t=4)
+            units = [(0, 0, HALF), (1, 0, HALF), (0, HALF, HALF), (1, HALF, CHUNK), (1, HALF + CHUNK, CHUNK)]
+            for n, (g, start, width) in enumerate(units):
+                cols = slice(start, start + width)
+                y = late.tile([P, 4, width], F32, name="y", tag="y", bufs=2)
+                for t in range(4):
+                    i = 4 * g + t
+                    picked = late.tile([P, width], F32, name="picked4", tag="picked4", bufs=6)
+                    nc.vector.tensor_copy(picked[:], pages[i][:].indirect(list4[:, start // 16 : (start + width) // 16]))
+                    bank = psum.tile([P, width], F32, name="enc_bank", tag="ph_bank", bufs=3)
+                    for b in range(2):
+                        nc.tensor.matmul_mx(
+                            out=bank[:],
+                            lhsT=w2_dealt[b][:, P * i : P * (i + 1)].bitcast(FP8X4),
+                            lhsT_scale=wscale_dealt[4 + 4 * b : P, P * i : P * (i + 1)],
+                            rhs=x_codes[b][:, cols].bitcast(FP8X4),
+                            rhs_scale=x_scales[b][:, cols],
+                            start=(b == 0), stop=(b == 1),
+                        )
+                    nc.vector.scalar_tensor_tensor(
+                        out=y[:, t, :], in0=picked[:], scalar=gn_sb[:, g, t : t + 1], in1=bank[:], op0=ALU.mult, op1=ALU.add
+                    )
+                nc.sync.dma_start(out=y_rows[g][:, :, cols], in_=y[:])
+                grouped = late.tile([P, 4 * width], BF16, name="y_grouped", tag="y_grouped", bufs=2, align_bytes=64)
+                interleave(nc.vector.tensor_copy if n == len(units) - 1 else nc.scalar.copy, grouped[:], y[:])
+                nc.vector.quantize_mx(out=y_codes[g][:, cols].bitcast(FP8X4), scales=y_scales[4 * g : P, cols], in_=grouped[:])
+                nc.sync.dma_start(
+                    out=out_1[g].rearrange("p m t -> p (m t)").bitcast(I32)[:, cols], in_=y_codes[g][:, cols].bitcast(I32)
+                )
+            for q in range(4):
+                queue = nc.scalar if q % 2 == 0 else nc.sync
+                queue.dma_start(
+                    out=out_2[:, 4 * q : 4 * q + 4, :].bitcast(I32), in_=y_scales[32 * q : 32 * q + 8, :].bitcast(I32)
+                )

@@ -25,9 +25,12 @@ TWO_PI = 2.0 * math.pi
 ROUNDER = 1.5 * 2.0**23
 
 
-def deal_and_round(copy, grouped, raw, first, count):
-    dst = grouped[:].rearrange("p (t mm m2 j) -> p mm j m2 t", t=4, m2=2, j=4)[:, first : first + count]
-    copy(out=dst, in_=raw[:].rearrange("p j (mm m2 t) -> p mm j m2 t", m2=2, t=4))
+def deal_and_round(copy, grouped, raw, pieces=1):
+    dst = grouped[:].rearrange("p (t mm m2 j) -> p mm j m2 t", t=4, m2=2, j=4)
+    src = raw[:].rearrange("p j (mm m2 t) -> p mm j m2 t", m2=2, t=4)
+    size = 64 // pieces
+    for k in range(pieces):
+        copy(out=dst[:, k * size : (k + 1) * size], in_=src[:, k * size : (k + 1) * size])
 
 
 def interleave(copy, grouped, planes):
@@ -55,8 +58,7 @@ def tile_list_blade_tip_page_kernel(
         gx_sb = keep.tile([P, 2, 4], F32, name="gx_sb")
         gn_sb = keep.tile([P, 2, 4], F32, name="gn_sb")
         pages = [keep.tile([P, T2], F32, name="page%d" % i) for i in range(8)]
-        wgs_first = keep.tile([P, 4, CHUNK], F32, name="wgs_first")
-        wgs_rest = keep.tile([P, 4, S - CHUNK], F32, name="wgs_rest")
+        wgs_sb = {}
         f_codes = [keep.tile([P, S], U32, name="f_codes%d" % h, align_bytes=64) for h in range(2)]
         f_scales = [keep.tile([P, S], U8, name="f_scales%d" % h, align_bytes=64) for h in range(2)]
         wc_codes = [keep.tile([P, 512], U32, name="wc_codes%d" % b, align_bytes=64) for b in range(2)]
@@ -69,6 +71,11 @@ def tile_list_blade_tip_page_kernel(
         wc_rows = wc.rearrange("(p j) c -> p j c", j=4)
 
         hs_tiles = {}
+
+        def load_wgs(c):
+            wgs_sb[c] = keep.tile([P, 4, CHUNK], F32, name="wgs_sb", tag="wgs_sb", bufs=2)
+            for q in range(4):
+                nc.sync.dma_start(out=wgs_sb[c][32 * q : 32 * (q + 1)], in_=wgs_rows[:, :, c * CHUNK : (c + 1) * CHUNK])
 
         def first_products(c):
             cols = slice(c * CHUNK, (c + 1) * CHUNK)
@@ -88,7 +95,7 @@ def tile_list_blade_tip_page_kernel(
                 nc.scalar.copy(out=hs[:], in_=bank[:])
                 hs_tiles[c, pair] = hs
 
-        def place_pair(c, pair):
+        def place_pair(c, pair, h=None):
             cols = slice(c * CHUNK, (c + 1) * CHUNK)
             bank = psum.tile([P, 2, CHUNK], F32, name="hc_bank", tag="hc_bank", bufs=3)
             for e in range(2):
@@ -101,14 +108,14 @@ def tile_list_blade_tip_page_kernel(
                     rhs_scale=f_scales[1][:, cols],
                     start=True, stop=True,
                 )
-            h = keep.tile([P, 2, CHUNK], F32, name="h", tag="h", bufs=2)
+            if h is None:
+                h = keep.tile([P, 2, CHUNK], F32, name="h", tag="h", bufs=2)
             nc.vector.tensor_tensor(out=h[:], in0=bank[:], in1=hs_tiles[c, pair][:], op=ALU.max)
             for e in range(2):
                 i = 2 * pair + e
                 t = i % 4
-                weight = wgs_first[:, t, :] if c == 0 else wgs_rest[:, t, (c - 1) * CHUNK : c * CHUNK]
                 places = list2[:, c * CHUNK // 16 : (c + 1) * CHUNK // 16]
-                nc.vector.tensor_tensor(pages[i][:].indirect(places), h[:, e, :], weight, ALU.mult)
+                nc.vector.tensor_tensor(pages[i][:].indirect(places), h[:, e, :], wgs_sb[c][:, t, :], ALU.mult)
 
         with tc.tile_pool(name="early", bufs=1) as early:
             tab_sb = [early.tile([P, T], U32, name="tab_sb%d" % a) for a in range(2)]
@@ -119,57 +126,55 @@ def tile_list_blade_tip_page_kernel(
             v_scales = early.tile([P, S], U8, name="v_scales", align_bytes=64)
             w1_codes = [early.tile([P, R], U32, name="w1_codes%d" % a, align_bytes=64) for a in range(2)]
             w1_scales = [early.tile([P, R], U8, name="w1_scales%d" % a, align_bytes=64) for a in range(2)]
-            w1_raw0 = early.tile([P, 4, R], F32, name="w1_raw0", tag="raw_a")
-            w1_raw1 = [early.tile([P, 4, R // 2], F32, name="w1_raw1_%d" % u) for u in range(2)]
+            w1_raw = [early.tile([P, 4, R], F32, name="w1_raw%d" % a) for a in range(2)]
             wc_raw0 = early.tile([P, 4, 512], F32, name="wc_raw0")
 
             nc.vector.memset(tab_scale_sb[:].bitcast(I32), 0)
             nc.gpsimd.memset(wscale_raw[:].bitcast(I32), 0)
             w1_rows = w1.rearrange("(a p j) c -> a p j c", a=2, j=4)
-            nc.sync.dma_start(list1[:], offs)
-            nc.sync.dma_start(out=gsc_sb[:], in_=gsc.rearrange("(h p t) -> p h t", h=2, t=4))
-            nc.sync.dma_start(list2[:], offs2)
-            nc.sync.dma_start(list3[:], offs3)
-            nc.sync.dma_start(list4[:], offs4)
-            nc.sync.dma_start(out=ws_raw[:].bitcast(I32), in_=ws_words[0].bitcast(I32))
-            for a in range(2):
+
+            def load_table(a):
                 nc.sync.dma_start(
                     out=tab_sb[a][:].bitcast(I32), in_=tab_words[a].rearrange("p t i -> p (t i)").bitcast(I32)
                 )
-            for q in range(4):
-                nc.scalar.dma_start(
-                    out=tab_scale_sb[32 * q : 32 * q + 8, :].bitcast(I32),
-                    in_=tab_scales[:, 4 * q : 4 * q + 4, :].bitcast(I32),
-                )
-            for q in range(4):
-                nc.scalar.dma_start(
+
+            def load_ws_scales(q):
+                nc.sync.dma_start(
                     out=wscale_raw[32 * q : 32 * q + 4, :].bitcast(I32),
                     in_=ws_scales[0, 4 * q : 4 * q + 4, :].bitcast(I32),
                 )
+
+            nc.sync.dma_start(list1[:], offs)
+            nc.sync.dma_start(out=w1_raw[0][:], in_=w1_rows[0])
             for q in range(4):
-                nc.gpsimd.dma_start(
-                    out=wscale_raw[32 * q + 4 : 32 * q + 12, :].bitcast(I32),
-                    in_=w2_scales[:, 4 * q : 4 * q + 4, :].bitcast(I32),
+                nc.sync.dma_start(
+                    out=tab_scale_sb[32 * q : 32 * q + 8, :].bitcast(I32),
+                    in_=tab_scales[:, 4 * q : 4 * q + 4, :].bitcast(I32),
                 )
-            nc.sync.dma_start(out=w1_raw0[:], in_=w1_rows[0])
-            for u in range(2):
-                nc.sync.dma_start(out=w1_raw1[u][:], in_=w1_rows[1][:, :, u * 256 : (u + 1) * 256])
+            nc.sync.dma_start(out=ws_raw[:].bitcast(I32), in_=ws_words[0].bitcast(I32))
+            nc.sync.dma_start(out=w1_raw[1][:], in_=w1_rows[1])
+            for q in range(4):
+                load_ws_scales(q)
+            load_table(0)
+            load_table(1)
             nc.sync.dma_start(out=wc_raw0[:], in_=wc_rows[:, :, 0:512])
             nc.sync.dma_start(out=pages[0][:], in_=page_rows[0, 0])
-            for q in range(4):
-                nc.sync.dma_start(out=wgs_first[32 * q : 32 * (q + 1)], in_=wgs_rows[:, :, 0:CHUNK])
-            for i in range(1, 3):
+            nc.sync.dma_start(out=gsc_sb[:], in_=gsc.rearrange("(h p t) -> p h t", h=2, t=4))
+            nc.sync.dma_start(list2[:], offs2)
+            load_wgs(0)
+            for i in range(1, 4):
                 nc.sync.dma_start(out=pages[i][:], in_=page_rows[i // 4, i % 4])
-
-            nc.vector.tensor_copy(v_codes[0][:], tab_sb[0][:].indirect(list1[:]))
-            nc.vector.tensor_copy(v_scales[:], tab_scale_sb[:].indirect(list1[:]))
-            nc.vector.tensor_copy(v_codes[1][:], tab_sb[1][:].indirect(list1[:]))
 
             w1_grouped = [
                 early.tile([P, 4 * R], BF16, name="w1_grouped%d" % a, tag="w_grouped", bufs=2, align_bytes=64)
                 for a in range(2)
             ]
-            deal_and_round(nc.scalar.copy, w1_grouped[0], w1_raw0, 0, 64)
+            deal_and_round(nc.scalar.copy, w1_grouped[0], w1_raw[0])
+            deal_and_round(nc.scalar.copy, w1_grouped[1], w1_raw[1])
+            nc.vector.tensor_copy(v_scales[:], tab_scale_sb[:].indirect(list1[:]))
+            for a in range(2):
+                nc.vector.quantize_mx(out=w1_codes[a][:].bitcast(FP8X4), scales=w1_scales[a][:], in_=w1_grouped[a][:])
+            nc.vector.tensor_copy(v_codes[0][:], tab_sb[0][:].indirect(list1[:]))
             nc.vector.tensor_copy(
                 out=ws_dealt[:].rearrange("p (b t m e) -> p b m t e", b=2, t=4, e=2),
                 in_=ws_raw[:].rearrange("p (b m t e) -> p b m t e", b=2, t=4, e=2),
@@ -179,16 +184,18 @@ def tile_list_blade_tip_page_kernel(
                 in_=wscale_raw[:].rearrange("p (b m t) -> p b m t", b=2, t=4),
             )
             for u in range(2):
-                deal_and_round(nc.vector.tensor_copy, w1_grouped[1], w1_raw1[u], 32 * u, 32)
-            for a in range(2):
-                nc.vector.quantize_mx(out=w1_codes[a][:].bitcast(FP8X4), scales=w1_scales[a][:], in_=w1_grouped[a][:])
+                nc.vector.tensor_copy(
+                    v_codes[1][:, u * HALF : (u + 1) * HALF],
+                    tab_sb[1][:].indirect(list1[:, u * HALF // 16 : (u + 1) * HALF // 16]),
+                )
 
-            wc_raw1 = early.tile([P, 4, 512], F32, name="wc_raw1", tag="raw_a")
+            wc_raw1 = early.tile([P, 4, 512], F32, name="wc_raw1")
             nc.sync.dma_start(out=wc_raw1[:], in_=wc_rows[:, :, 512:1024])
-            for i in range(3, 8):
+            for i in range(4, 8):
                 nc.sync.dma_start(out=pages[i][:], in_=page_rows[i // 4, i % 4])
-            for q in range(4):
-                nc.sync.dma_start(out=wgs_rest[32 * q : 32 * (q + 1)], in_=wgs_rows[:, :, CHUNK:S])
+            load_wgs(1)
+            nc.sync.dma_start(list3[:], offs3)
+            nc.sync.dma_start(list4[:], offs4)
             nc.sync.dma_start(out=gx_sb[:], in_=gx.rearrange("(b p t) -> p b t", b=2, t=4))
             nc.sync.dma_start(out=gn_sb[:], in_=gn.rearrange("(b p t) -> p b t", b=2, t=4))
 
@@ -206,50 +213,17 @@ def tile_list_blade_tip_page_kernel(
             def scratch(name, dtype, bufs):
                 return early.tile([P, 4 * CHUNK], dtype, name=name, tag=name, bufs=bufs, align_bytes=64)
 
-            def sine_and_cosine(sine, size, cosine, frac):
-                nc.scalar.activation(out=sine, in_=frac, func=ACT.Sin, scale=-TWO_PI)
+            def cosine_of(cosine, size, frac):
                 nc.scalar.activation(out=size, in_=frac, func=ACT.Abs)
                 nc.scalar.activation(out=cosine, in_=size, func=ACT.Sin, scale=-TWO_PI, bias=math.pi / 2)
 
-            def quantize_wc(b, copy, raw):
+            def quantize_wc(b, copy, raw, pieces):
                 grouped = early.tile([P, 4 * 512], BF16, name="wc_grouped", tag="w_grouped", bufs=2, align_bytes=64)
-                deal_and_round(copy, grouped, raw, 0, 64)
+                deal_and_round(copy, grouped, raw, pieces)
                 nc.vector.quantize_mx(out=wc_codes[b][:].bitcast(FP8X4), scales=wc_scales[b][:], in_=grouped[:])
 
-            turns, whole, frac = scratch("turns", F32, 1), scratch("whole", I32, 1), scratch("frac", F32, 2)
-            sine, size, cosine = scratch("sine", F32, 1), scratch("size", F32, 1), scratch("cosine", F32, 1)
-            grouped0 = [scratch("f_grouped%d" % h, BF16, 2) for h in range(2)]
-            for u in range(2):
-                bank = psum.tile([P, 4, P], F32, name="ph_bank0", tag="ph_bank", bufs=3)
-                for t in range(4):
-                    phases(bank[:, t, :], t, slice(u * P, (u + 1) * P))
-                part = slice(u * 4 * P, (u + 1) * 4 * P)
-                nc.scalar.activation(
-                    out=turns[:, part].rearrange("p (n t) -> p n t", t=4), in_=bank[:].rearrange("p t n -> p n t"),
-                    func=ACT.Copy, scale=1.0 / TWO_PI,
-                )
-                nc.vector.tensor_scalar(out=whole[:, part], in0=turns[:, part], scalar1=ROUNDER, scalar2=None, op0=ALU.add)
-                nc.vector.scalar_tensor_tensor(
-                    out=frac[:, part], in0=whole[:, part], scalar=ROUNDER, in1=turns[:, part],
-                    op0=ALU.subtract, op1=ALU.subtract,
-                )
-                sine_and_cosine(sine[:, part], size[:, part], cosine[:, part], frac[:, part])
-            quantize_wc(0, nc.vector.tensor_copy, wc_raw0)
-            for u in range(2):
-                part = slice(u * 4 * P, (u + 1) * 4 * P)
-                for h, values in enumerate((sine, cosine)):
-                    nc.vector.tensor_tensor(
-                        out=grouped0[h][:, part].rearrange("p (n t) -> p n t", t=4),
-                        in0=values[:, part].rearrange("p (n t) -> p n t", t=4),
-                        in1=gsc_sb[:, h : h + 1, :].to_broadcast([P, P, 4]),
-                        op=ALU.mult,
-                    )
-            for h in range(2):
-                nc.vector.quantize_mx(
-                    out=f_codes[h][:, 0:CHUNK].bitcast(FP8X4), scales=f_scales[h][:, 0:CHUNK], in_=grouped0[h][:]
-                )
-
             fracs = {}
+            shared = early.tile([P, 2 * CHUNK], F32, name="shared", align_bytes=64)
 
             def reduce_phases(c):
                 turns, whole, frac = scratch("turns", F32, 1), scratch("whole", I32, 1), scratch("frac", F32, 2)
@@ -269,7 +243,8 @@ def tile_list_blade_tip_page_kernel(
 
             def features(c):
                 sine, size, cosine = scratch("sine", F32, 1), scratch("size", F32, 1), scratch("cosine", F32, 1)
-                sine_and_cosine(sine[:], size[:], cosine[:], fracs[c][:])
+                nc.scalar.activation(out=sine[:], in_=fracs[c][:], func=ACT.Sin, scale=-TWO_PI)
+                cosine_of(cosine[:], size[:], fracs[c][:])
                 result = []
                 for h, values in enumerate((sine, cosine)):
                     planes = early.tile([P, 4, CHUNK], BF16, name="f_planes%d" % h, tag="f_planes%d" % h)
@@ -278,8 +253,8 @@ def tile_list_blade_tip_page_kernel(
                             out=planes[:, t, :], in_=values[:, t * CHUNK : (t + 1) * CHUNK], func=ACT.Copy,
                             scale=gsc_sb[:, h, t : t + 1],
                         )
-                    grouped = scratch("f_grouped%d" % h, BF16, 2)
-                    interleave(nc.scalar.copy, grouped[:], planes[:])
+                    grouped = shared[:].bitcast(BF16) if h == 0 else scratch("f_grouped1", BF16, 2)[:]
+                    interleave(nc.scalar.copy, grouped, planes[:])
                     result.append(grouped)
                 return result
 
@@ -290,20 +265,57 @@ def tile_list_blade_tip_page_kernel(
                         out=f_codes[h][:, cols].bitcast(FP8X4), scales=f_scales[h][:, cols], in_=grouped[h][:]
                     )
 
+            turns, whole, frac = scratch("turns", F32, 1), scratch("whole", I32, 1), scratch("frac", F32, 2)
+            sine, size, cosine = scratch("sine", F32, 1), scratch("size", F32, 1), scratch("cosine", F32, 1)
+            grouped0 = [shared[:].bitcast(BF16), scratch("f_grouped1", BF16, 2)]
+            for u in range(2):
+                bank = psum.tile([P, 4, P], F32, name="ph_bank0", tag="ph_bank", bufs=3)
+                for t in range(4):
+                    phases(bank[:, t, :], t, slice(u * P, (u + 1) * P))
+                part = slice(u * 4 * P, (u + 1) * 4 * P)
+                nc.scalar.activation(
+                    out=turns[:, part].rearrange("p (n t) -> p n t", t=4), in_=bank[:].rearrange("p t n -> p n t"),
+                    func=ACT.Copy, scale=1.0 / TWO_PI,
+                )
+                nc.vector.tensor_scalar(out=whole[:, part], in0=turns[:, part], scalar1=ROUNDER, scalar2=None, op0=ALU.add)
+                nc.vector.scalar_tensor_tensor(
+                    out=frac[:, part], in0=whole[:, part], scalar=ROUNDER, in1=turns[:, part],
+                    op0=ALU.subtract, op1=ALU.subtract,
+                )
+                nc.scalar.activation(out=sine[:, part], in_=frac[:, part], func=ACT.Sin, scale=-TWO_PI)
+            for u in range(2):
+                part = slice(u * 4 * P, (u + 1) * 4 * P)
+                cosine_of(cosine[:, part], size[:, part], frac[:, part])
+            for h, values in enumerate((sine, cosine)):
+                for u in range(2):
+                    part = slice(u * 4 * P, (u + 1) * 4 * P)
+                    nc.vector.tensor_tensor(
+                        out=grouped0[h][:, part].rearrange("p (n t) -> p n t", t=4),
+                        in0=values[:, part].rearrange("p (n t) -> p n t", t=4),
+                        in1=gsc_sb[:, h : h + 1, :].to_broadcast([P, P, 4]),
+                        op=ALU.mult,
+                    )
+                nc.vector.quantize_mx(
+                    out=f_codes[h][:, 0:CHUNK].bitcast(FP8X4), scales=f_scales[h][:, 0:CHUNK], in_=grouped0[h][:]
+                )
+
+            quantize_wc(0, nc.vector.tensor_copy, wc_raw0, 1)
             first_products(0)
             reduce_phases(1)
             for c in range(CHUNKS - 1):
                 place_pair(c, 0)
                 if c == 0:
-                    quantize_wc(1, nc.scalar.copy, wc_raw1)
+                    quantize_wc(1, nc.scalar.copy, wc_raw1, 1)
                 grouped = features(c + 1)
+                if c + 2 < CHUNKS:
+                    reduce_phases(c + 2)
                 place_pair(c, 1)
                 place_pair(c, 2)
                 quantize_features(c + 1, grouped)
                 first_products(c + 1)
+                place_pair(c, 3, shared[:].rearrange("p (e n) -> p e n", e=2) if c else None)
                 if c + 2 < CHUNKS:
-                    reduce_phases(c + 2)
-                place_pair(c, 3)
+                    load_wgs(c + 2)
 
         with tc.tile_pool(name="late", bufs=1) as late:
             w2_raw = [late.tile([P, H], U32, name="w2_raw%d" % a) for a in range(2)]
@@ -316,6 +328,19 @@ def tile_list_blade_tip_page_kernel(
                 nc.sync.dma_start(
                     out=w2_raw[a][:].bitcast(I32), in_=w2_words[a].rearrange("p c i -> p (c i)").bitcast(I32)
                 )
+
+            w2_scale_raw = late.tile([P, H], U8, name="w2_scale_raw")
+            w2_scale_dealt = late.tile([P, H], U8, name="w2_scale_dealt", align_bytes=64)
+            nc.gpsimd.memset(w2_scale_raw[:].bitcast(I32), 0)
+            for q in range(4):
+                nc.sync.dma_start(
+                    out=w2_scale_raw[32 * q : 32 * q + 8, :].bitcast(I32),
+                    in_=w2_scales[:, 4 * q : 4 * q + 4, :].bitcast(I32),
+                )
+            nc.vector.tensor_copy(
+                out=w2_scale_dealt[:].rearrange("p (g t m) -> p g m t", g=2, t=4),
+                in_=w2_scale_raw[:].rearrange("p (g m t) -> p g m t", g=2, t=4),
+            )
 
             for b in range(2):
                 place_pair(CHUNKS - 1, 2 * b)
@@ -351,7 +376,7 @@ def tile_list_blade_tip_page_kernel(
                         nc.tensor.matmul_mx(
                             out=bank[:],
                             lhsT=w2_dealt[b][:, P * i : P * (i + 1)].bitcast(FP8X4),
-                            lhsT_scale=wscale_dealt[4 + 4 * b : P, P * i : P * (i + 1)],
+                            lhsT_scale=w2_scale_dealt[4 * b : P, P * i : P * (i + 1)],
                             rhs=x_codes[b][:, cols].bitcast(FP8X4),
                             rhs_scale=x_scales[b][:, cols],
                             start=(b == 0), stop=(b == 1),

@@ -18,6 +18,7 @@ P = 128
 K, T, S, R, H, T2 = 1024, 4096, 1024, 512, 1024, 2048
 FLOPS = 2 * (K * R * S + 2 * R * H * S + H * H * S)
 
+GROUP = 512
 CHUNK = 256
 CHUNKS = S // CHUNK
 HALF = S // 2
@@ -25,18 +26,18 @@ TWO_PI = 2.0 * math.pi
 ROUNDER = 1.5 * 2.0**23
 
 
-def deal_and_round(copy, grouped, raw, pieces=1):
-    dst = grouped[:].rearrange("p (t mm m2 j) -> p mm j m2 t", t=4, m2=2, j=4)
-    src = raw[:].rearrange("p j (mm m2 t) -> p mm j m2 t", m2=2, t=4)
-    size = 64 // pieces
-    for k in range(pieces):
-        copy(out=dst[:, k * size : (k + 1) * size], in_=src[:, k * size : (k + 1) * size])
+def entries(places, start, count):
+    return places[:, start // 16 : (start + count) // 16]
 
 
-def interleave(copy, grouped, planes):
+def deal_and_round(copy, grouped, raw):
+    copy(out=grouped[:].rearrange("p (t m j) -> p m t j", t=4, j=4), in_=raw[:].rearrange("p j (m t) -> p m t j", t=4))
+
+
+def interleave(copy, grouped, tiles):
     copy(
         out=grouped.rearrange("p (c i t) -> p c t i", i=4, t=4),
-        in_=planes.rearrange("p t (c i) -> p c t i", i=4),
+        in_=tiles.rearrange("p t (c i) -> p c t i", i=4),
     )
 
 
@@ -58,26 +59,34 @@ def tile_list_blade_tip_page_kernel(
         gx_sb = keep.tile([P, 2, 4], F32, name="gx_sb")
         gn_sb = keep.tile([P, 2, 4], F32, name="gn_sb")
         pages = [keep.tile([P, T2], F32, name="page%d" % i) for i in range(8)]
-        wgs_sb = {}
-        f_codes = [keep.tile([P, S], U32, name="f_codes%d" % h, align_bytes=64) for h in range(2)]
-        f_scales = [keep.tile([P, S], U8, name="f_scales%d" % h, align_bytes=64) for h in range(2)]
-        wc_codes = [keep.tile([P, 512], U32, name="wc_codes%d" % b, align_bytes=64) for b in range(2)]
-        wc_scales = [keep.tile([P, 512], U8, name="wc_scales%d" % b, align_bytes=64) for b in range(2)]
+        f_codes = [keep.tile([P, S], U32, name="f_codes%d" % f, align_bytes=64) for f in range(2)]
+        f_scales = [keep.tile([P, S], U8, name="f_scales%d" % f, align_bytes=64) for f in range(2)]
+        wc_codes = [keep.tile([P, GROUP], U32, name="wc_codes%d" % g, align_bytes=64) for g in range(2)]
+        wc_scales = [keep.tile([P, GROUP], U8, name="wc_scales%d" % g, align_bytes=64) for g in range(2)]
         ws_dealt = keep.tile([P, 2 * H], U8, name="ws_dealt", align_bytes=64)
-        wscale_dealt = keep.tile([P, H], U8, name="wscale_dealt", align_bytes=64)
+        ws_scale_dealt = keep.tile([P, H], U8, name="ws_scale_dealt", align_bytes=64)
 
-        page_rows = page0.rearrange("(b p t) c -> b t p c", b=2, t=4)
+        warm = keep.tile([P, 2], F32, name="warm")
+        nc.gpsimd.memset(warm[:, 0:1], 0.0)
+        nc.scalar.activation(out=warm[:, 1:2], in_=warm[:, 0:1], func=ACT.Sin)
+
+        page_rows = page0.rearrange("(g p t) c -> g t p c", g=2, t=4)
         wgs_rows = wgs.rearrange("(q t) j -> q t j", t=4)
         wc_rows = wc.rearrange("(p j) c -> p j c", j=4)
 
-        hs_tiles = {}
+        wgs_sb = {}
+        hs_sb = {}
+        shared = keep.tile([P, 2 * CHUNK], F32, name="shared", align_bytes=64)
+
+        def load_page(i):
+            nc.sync.dma_start(out=pages[i][:], in_=page_rows[i // 4, i % 4])
 
         def load_wgs(c):
             wgs_sb[c] = keep.tile([P, 4, CHUNK], F32, name="wgs_sb", tag="wgs_sb", bufs=2)
-            for q in range(4):
+            for q in (0, 2, 1, 3):
                 nc.sync.dma_start(out=wgs_sb[c][32 * q : 32 * (q + 1)], in_=wgs_rows[:, :, c * CHUNK : (c + 1) * CHUNK])
 
-        def first_products(c):
+        def sine_products(c):
             cols = slice(c * CHUNK, (c + 1) * CHUNK)
             for pair in range(4):
                 bank = psum.tile([P, 2, CHUNK], F32, name="hs_bank", tag="hs_bank", bufs=2)
@@ -85,65 +94,54 @@ def tile_list_blade_tip_page_kernel(
                     i = 2 * pair + e
                     nc.tensor.matmul_mx(
                         out=bank[:, e, :],
-                        lhsT=ws_dealt[:, 256 * i : 256 * (i + 1)].bitcast(FP4X4),
-                        lhsT_scale=wscale_dealt[:, P * i : P * (i + 1)],
+                        lhsT=ws_dealt[:, 2 * P * i : 2 * P * (i + 1)].bitcast(FP4X4),
+                        lhsT_scale=ws_scale_dealt[:, P * i : P * (i + 1)],
                         rhs=f_codes[0][:, cols].bitcast(FP8X4),
                         rhs_scale=f_scales[0][:, cols],
                         start=True, stop=True,
                     )
-                hs = keep.tile([P, 2, CHUNK], F32, name="hs", tag="hs", bufs=4)
-                nc.scalar.copy(out=hs[:], in_=bank[:])
-                hs_tiles[c, pair] = hs
+                hs_sb[c, pair] = keep.tile([P, 2, CHUNK], F32, name="hs_sb", tag="hs_sb", bufs=4)
+                nc.scalar.copy(out=hs_sb[c, pair][:], in_=bank[:])
 
-        def place_pair(c, pair, h=None):
+        def place_pair(c, pair):
             cols = slice(c * CHUNK, (c + 1) * CHUNK)
             bank = psum.tile([P, 2, CHUNK], F32, name="hc_bank", tag="hc_bank", bufs=3)
             for e in range(2):
-                b, t = divmod(2 * pair + e, 4)
+                g, t = divmod(2 * pair + e, 4)
                 nc.tensor.matmul_mx(
                     out=bank[:, e, :],
-                    lhsT=wc_codes[b][:, P * t : P * (t + 1)].bitcast(FP8X4),
-                    lhsT_scale=wc_scales[b][:, P * t : P * (t + 1)],
+                    lhsT=wc_codes[g][:, P * t : P * (t + 1)].bitcast(FP8X4),
+                    lhsT_scale=wc_scales[g][:, P * t : P * (t + 1)],
                     rhs=f_codes[1][:, cols].bitcast(FP8X4),
                     rhs_scale=f_scales[1][:, cols],
                     start=True, stop=True,
                 )
-            if h is None:
+            if (c, pair) == (CHUNKS - 2, 3):
+                h = shared[:].rearrange("p (e n) -> p e n", e=2)
+            else:
                 h = keep.tile([P, 2, CHUNK], F32, name="h", tag="h", bufs=2)
-            nc.vector.tensor_tensor(out=h[:], in0=bank[:], in1=hs_tiles[c, pair][:], op=ALU.max)
+            nc.vector.tensor_tensor(out=h[:], in0=bank[:], in1=hs_sb[c, pair][:], op=ALU.max)
             for e in range(2):
                 i = 2 * pair + e
-                t = i % 4
-                places = list2[:, c * CHUNK // 16 : (c + 1) * CHUNK // 16]
-                nc.vector.tensor_tensor(pages[i][:].indirect(places), h[:, e, :], wgs_sb[c][:, t, :], ALU.mult)
+                window = pages[i][:].indirect(entries(list2, c * CHUNK, CHUNK))
+                nc.vector.tensor_tensor(window, h[:, e, :], wgs_sb[c][:, i % 4, :], ALU.mult)
 
         with tc.tile_pool(name="early", bufs=1) as early:
             tab_sb = [early.tile([P, T], U32, name="tab_sb%d" % a) for a in range(2)]
             tab_scale_sb = early.tile([P, T], U8, name="tab_scale_sb")
-            wscale_raw = early.tile([P, H], U8, name="wscale_raw")
+            ws_scale_raw = early.tile([P, H], U8, name="ws_scale_raw")
             ws_raw = early.tile([P, 2 * H], U8, name="ws_raw")
             v_codes = [early.tile([P, S], U32, name="v_codes%d" % a, align_bytes=64) for a in range(2)]
             v_scales = early.tile([P, S], U8, name="v_scales", align_bytes=64)
             w1_codes = [early.tile([P, R], U32, name="w1_codes%d" % a, align_bytes=64) for a in range(2)]
             w1_scales = [early.tile([P, R], U8, name="w1_scales%d" % a, align_bytes=64) for a in range(2)]
             w1_raw = [early.tile([P, 4, R], F32, name="w1_raw%d" % a) for a in range(2)]
-            wc_raw0 = early.tile([P, 4, 512], F32, name="wc_raw0")
+            wc_raw0 = early.tile([P, 4, GROUP], F32, name="wc_raw0")
 
             nc.vector.memset(tab_scale_sb[:].bitcast(I32), 0)
-            nc.gpsimd.memset(wscale_raw[:].bitcast(I32), 0)
+            nc.gpsimd.memset(ws_scale_raw[:].bitcast(I32), 0)
+
             w1_rows = w1.rearrange("(a p j) c -> a p j c", a=2, j=4)
-
-            def load_table(a):
-                nc.sync.dma_start(
-                    out=tab_sb[a][:].bitcast(I32), in_=tab_words[a].rearrange("p t i -> p (t i)").bitcast(I32)
-                )
-
-            def load_ws_scales(q):
-                nc.sync.dma_start(
-                    out=wscale_raw[32 * q : 32 * q + 4, :].bitcast(I32),
-                    in_=ws_scales[0, 4 * q : 4 * q + 4, :].bitcast(I32),
-                )
-
             nc.sync.dma_start(list1[:], offs)
             nc.sync.dma_start(out=w1_raw[0][:], in_=w1_rows[0])
             for q in range(4):
@@ -154,50 +152,52 @@ def tile_list_blade_tip_page_kernel(
             nc.sync.dma_start(out=ws_raw[:].bitcast(I32), in_=ws_words[0].bitcast(I32))
             nc.sync.dma_start(out=w1_raw[1][:], in_=w1_rows[1])
             for q in range(4):
-                load_ws_scales(q)
-            load_table(0)
-            load_table(1)
-            nc.sync.dma_start(out=wc_raw0[:], in_=wc_rows[:, :, 0:512])
-            nc.sync.dma_start(out=pages[0][:], in_=page_rows[0, 0])
-            nc.sync.dma_start(out=gsc_sb[:], in_=gsc.rearrange("(h p t) -> p h t", h=2, t=4))
+                nc.sync.dma_start(
+                    out=ws_scale_raw[32 * q : 32 * q + 4, :].bitcast(I32),
+                    in_=ws_scales[0, 4 * q : 4 * q + 4, :].bitcast(I32),
+                )
+            for a in range(2):
+                nc.sync.dma_start(
+                    out=tab_sb[a][:].bitcast(I32), in_=tab_words[a].rearrange("p t i -> p (t i)").bitcast(I32)
+                )
+            nc.sync.dma_start(out=wc_raw0[:], in_=wc_rows[:, :, 0:GROUP])
+            load_page(0)
+            nc.sync.dma_start(out=gsc_sb[:], in_=gsc.rearrange("(f p t) -> p f t", f=2, t=4))
             nc.sync.dma_start(list2[:], offs2)
             load_wgs(0)
             for i in range(1, 4):
-                nc.sync.dma_start(out=pages[i][:], in_=page_rows[i // 4, i % 4])
+                load_page(i)
 
             w1_grouped = [
                 early.tile([P, 4 * R], BF16, name="w1_grouped%d" % a, tag="w_grouped", bufs=2, align_bytes=64)
                 for a in range(2)
             ]
-            deal_and_round(nc.scalar.copy, w1_grouped[0], w1_raw[0])
-            deal_and_round(nc.scalar.copy, w1_grouped[1], w1_raw[1])
+            for a in range(2):
+                deal_and_round(nc.scalar.copy, w1_grouped[a], w1_raw[a])
             nc.vector.tensor_copy(v_scales[:], tab_scale_sb[:].indirect(list1[:]))
             for a in range(2):
                 nc.vector.quantize_mx(out=w1_codes[a][:].bitcast(FP8X4), scales=w1_scales[a][:], in_=w1_grouped[a][:])
             nc.vector.tensor_copy(v_codes[0][:], tab_sb[0][:].indirect(list1[:]))
             nc.vector.tensor_copy(
-                out=ws_dealt[:].rearrange("p (b t m e) -> p b m t e", b=2, t=4, e=2),
-                in_=ws_raw[:].rearrange("p (b m t e) -> p b m t e", b=2, t=4, e=2),
+                out=ws_dealt[:].rearrange("p (g t m e) -> p g t m e", g=2, t=4, e=2),
+                in_=ws_raw[:].rearrange("p (g m t e) -> p g t m e", g=2, t=4, e=2),
             )
             nc.vector.tensor_copy(
-                out=wscale_dealt[:].rearrange("p (b t m) -> p b m t", b=2, t=4),
-                in_=wscale_raw[:].rearrange("p (b m t) -> p b m t", b=2, t=4),
+                out=ws_scale_dealt[:].rearrange("p (g t m) -> p g t m", g=2, t=4),
+                in_=ws_scale_raw[:].rearrange("p (g m t) -> p g t m", g=2, t=4),
             )
-            for u in range(2):
-                nc.vector.tensor_copy(
-                    v_codes[1][:, u * HALF : (u + 1) * HALF],
-                    tab_sb[1][:].indirect(list1[:, u * HALF // 16 : (u + 1) * HALF // 16]),
-                )
+            for start in (0, HALF):
+                nc.vector.tensor_copy(v_codes[1][:, start : start + HALF], tab_sb[1][:].indirect(entries(list1, start, HALF)))
 
-            wc_raw1 = early.tile([P, 4, 512], F32, name="wc_raw1")
-            nc.sync.dma_start(out=wc_raw1[:], in_=wc_rows[:, :, 512:1024])
+            wc_raw1 = early.tile([P, 4, GROUP], F32, name="wc_raw1")
+            nc.sync.dma_start(out=wc_raw1[:], in_=wc_rows[:, :, GROUP : 2 * GROUP])
             for i in range(4, 8):
-                nc.sync.dma_start(out=pages[i][:], in_=page_rows[i // 4, i % 4])
+                load_page(i)
             load_wgs(1)
             nc.sync.dma_start(list3[:], offs3)
             nc.sync.dma_start(list4[:], offs4)
-            nc.sync.dma_start(out=gx_sb[:], in_=gx.rearrange("(b p t) -> p b t", b=2, t=4))
-            nc.sync.dma_start(out=gn_sb[:], in_=gn.rearrange("(b p t) -> p b t", b=2, t=4))
+            nc.sync.dma_start(out=gx_sb[:], in_=gx.rearrange("(g p t) -> p g t", g=2, t=4))
+            nc.sync.dma_start(out=gn_sb[:], in_=gn.rearrange("(g p t) -> p g t", g=2, t=4))
 
             def phases(out, t, cols):
                 for a in range(2):
@@ -213,20 +213,31 @@ def tile_list_blade_tip_page_kernel(
             def scratch(name, dtype, bufs):
                 return early.tile([P, 4 * CHUNK], dtype, name=name, tag=name, bufs=bufs, align_bytes=64)
 
+            def fraction(frac, whole, turns):
+                nc.vector.scalar_tensor_tensor(
+                    out=frac, in0=whole, scalar=ROUNDER, in1=turns, op0=ALU.subtract, op1=ALU.subtract
+                )
+
+            def sine_of(sine, frac):
+                nc.scalar.activation(out=sine, in_=frac, func=ACT.Sin, scale=-TWO_PI)
+
             def cosine_of(cosine, size, frac):
                 nc.scalar.activation(out=size, in_=frac, func=ACT.Abs)
                 nc.scalar.activation(out=cosine, in_=size, func=ACT.Sin, scale=-TWO_PI, bias=math.pi / 2)
 
-            def quantize_wc(b, copy, raw, pieces):
-                grouped = early.tile([P, 4 * 512], BF16, name="wc_grouped", tag="w_grouped", bufs=2, align_bytes=64)
-                deal_and_round(copy, grouped, raw, pieces)
-                nc.vector.quantize_mx(out=wc_codes[b][:].bitcast(FP8X4), scales=wc_scales[b][:], in_=grouped[:])
+            def quantize_wc(g, copy, raw):
+                grouped = early.tile([P, 4 * GROUP], BF16, name="wc_grouped", tag="w_grouped", bufs=2, align_bytes=64)
+                deal_and_round(copy, grouped, raw)
+                nc.vector.quantize_mx(out=wc_codes[g][:].bitcast(FP8X4), scales=wc_scales[g][:], in_=grouped[:])
+
+            def quantize_features(c, f, grouped):
+                cols = slice(c * CHUNK, (c + 1) * CHUNK)
+                nc.vector.quantize_mx(out=f_codes[f][:, cols].bitcast(FP8X4), scales=f_scales[f][:, cols], in_=grouped)
 
             fracs = {}
-            shared = early.tile([P, 2 * CHUNK], F32, name="shared", align_bytes=64)
 
             def reduce_phases(c):
-                turns, whole, frac = scratch("turns", F32, 1), scratch("whole", I32, 1), scratch("frac", F32, 2)
+                turns, whole, fracs[c] = scratch("turns", F32, 1), scratch("whole", I32, 1), scratch("frac", F32, 2)
                 for u in range(2):
                     bank = psum.tile([P, 2, CHUNK], F32, name="ph_bank", tag="ph_bank", bufs=3)
                     for e in range(2):
@@ -236,94 +247,80 @@ def tile_list_blade_tip_page_kernel(
                         func=ACT.Copy, scale=1.0 / TWO_PI,
                     )
                 nc.scalar.activation(out=whole[:].bitcast(U32), in_=turns[:], func=ACT.Copy, bias=ROUNDER)
-                nc.vector.scalar_tensor_tensor(
-                    out=frac[:], in0=whole[:], scalar=ROUNDER, in1=turns[:], op0=ALU.subtract, op1=ALU.subtract
-                )
-                fracs[c] = frac
+                fraction(fracs[c][:], whole[:], turns[:])
 
             def features(c):
                 sine, size, cosine = scratch("sine", F32, 1), scratch("size", F32, 1), scratch("cosine", F32, 1)
-                nc.scalar.activation(out=sine[:], in_=fracs[c][:], func=ACT.Sin, scale=-TWO_PI)
+                sine_of(sine[:], fracs[c][:])
                 cosine_of(cosine[:], size[:], fracs[c][:])
-                result = []
-                for h, values in enumerate((sine, cosine)):
-                    planes = early.tile([P, 4, CHUNK], BF16, name="f_planes%d" % h, tag="f_planes%d" % h)
+                grouped = []
+                for f, values in enumerate((sine, cosine)):
+                    tiles = early.tile([P, 4, CHUNK], BF16, name="f_tiles%d" % f, tag="f_tiles%d" % f)
                     for t in range(4):
                         nc.scalar.activation(
-                            out=planes[:, t, :], in_=values[:, t * CHUNK : (t + 1) * CHUNK], func=ACT.Copy,
-                            scale=gsc_sb[:, h, t : t + 1],
+                            out=tiles[:, t, :], in_=values[:, t * CHUNK : (t + 1) * CHUNK], func=ACT.Copy,
+                            scale=gsc_sb[:, f, t : t + 1],
                         )
-                    grouped = shared[:].bitcast(BF16) if h == 0 else scratch("f_grouped1", BF16, 2)[:]
-                    interleave(nc.scalar.copy, grouped, planes[:])
-                    result.append(grouped)
-                return result
-
-            def quantize_features(c, grouped):
-                cols = slice(c * CHUNK, (c + 1) * CHUNK)
-                for h in range(2):
-                    nc.vector.quantize_mx(
-                        out=f_codes[h][:, cols].bitcast(FP8X4), scales=f_scales[h][:, cols], in_=grouped[h][:]
-                    )
+                    if (c, f) == (CHUNKS - 1, 1):
+                        grouped.append(shared[:].bitcast(BF16))
+                    else:
+                        grouped.append(scratch("f_grouped%d" % f, BF16, 2)[:])
+                    interleave(nc.scalar.copy, grouped[f], tiles[:])
+                return grouped
 
             turns, whole, frac = scratch("turns", F32, 1), scratch("whole", I32, 1), scratch("frac", F32, 2)
             sine, size, cosine = scratch("sine", F32, 1), scratch("size", F32, 1), scratch("cosine", F32, 1)
-            grouped0 = [shared[:].bitcast(BF16), scratch("f_grouped1", BF16, 2)]
-            for u in range(2):
+            grouped = [scratch("f_grouped%d" % f, BF16, 2) for f in range(2)]
+            parts = [slice(u * 4 * P, (u + 1) * 4 * P) for u in range(CHUNK // P)]
+            for u, part in enumerate(parts):
                 bank = psum.tile([P, 4, P], F32, name="ph_bank0", tag="ph_bank", bufs=3)
                 for t in range(4):
                     phases(bank[:, t, :], t, slice(u * P, (u + 1) * P))
-                part = slice(u * 4 * P, (u + 1) * 4 * P)
                 nc.scalar.activation(
                     out=turns[:, part].rearrange("p (n t) -> p n t", t=4), in_=bank[:].rearrange("p t n -> p n t"),
                     func=ACT.Copy, scale=1.0 / TWO_PI,
                 )
                 nc.vector.tensor_scalar(out=whole[:, part], in0=turns[:, part], scalar1=ROUNDER, scalar2=None, op0=ALU.add)
-                nc.vector.scalar_tensor_tensor(
-                    out=frac[:, part], in0=whole[:, part], scalar=ROUNDER, in1=turns[:, part],
-                    op0=ALU.subtract, op1=ALU.subtract,
-                )
-                nc.scalar.activation(out=sine[:, part], in_=frac[:, part], func=ACT.Sin, scale=-TWO_PI)
-            for u in range(2):
-                part = slice(u * 4 * P, (u + 1) * 4 * P)
+                fraction(frac[:, part], whole[:, part], turns[:, part])
+                sine_of(sine[:, part], frac[:, part])
+            for part in parts:
                 cosine_of(cosine[:, part], size[:, part], frac[:, part])
-            for h, values in enumerate((sine, cosine)):
-                for u in range(2):
-                    part = slice(u * 4 * P, (u + 1) * 4 * P)
+            for f, values in enumerate((sine, cosine)):
+                for part in parts:
                     nc.vector.tensor_tensor(
-                        out=grouped0[h][:, part].rearrange("p (n t) -> p n t", t=4),
+                        out=grouped[f][:, part].rearrange("p (n t) -> p n t", t=4),
                         in0=values[:, part].rearrange("p (n t) -> p n t", t=4),
-                        in1=gsc_sb[:, h : h + 1, :].to_broadcast([P, P, 4]),
+                        in1=gsc_sb[:, f : f + 1, :].to_broadcast([P, P, 4]),
                         op=ALU.mult,
                     )
-                nc.vector.quantize_mx(
-                    out=f_codes[h][:, 0:CHUNK].bitcast(FP8X4), scales=f_scales[h][:, 0:CHUNK], in_=grouped0[h][:]
-                )
-
-            quantize_wc(0, nc.vector.tensor_copy, wc_raw0, 1)
-            first_products(0)
+                quantize_features(0, f, grouped[f][:])
+            quantize_wc(0, nc.vector.tensor_copy, wc_raw0)
+            sine_products(0)
             reduce_phases(1)
+
             for c in range(CHUNKS - 1):
                 place_pair(c, 0)
                 if c == 0:
-                    quantize_wc(1, nc.scalar.copy, wc_raw1, 1)
+                    quantize_wc(1, nc.scalar.copy, wc_raw1)
                 grouped = features(c + 1)
                 if c + 2 < CHUNKS:
                     reduce_phases(c + 2)
                 place_pair(c, 1)
                 place_pair(c, 2)
-                quantize_features(c + 1, grouped)
-                first_products(c + 1)
-                place_pair(c, 3, shared[:].rearrange("p (e n) -> p e n", e=2) if c else None)
+                for f in range(2):
+                    quantize_features(c + 1, f, grouped[f])
+                sine_products(c + 1)
+                place_pair(c, 3)
                 if c + 2 < CHUNKS:
                     load_wgs(c + 2)
 
         with tc.tile_pool(name="late", bufs=1) as late:
             w2_raw = [late.tile([P, H], U32, name="w2_raw%d" % a) for a in range(2)]
             w2_dealt = [late.tile([P, H], U32, name="w2_dealt%d" % a, align_bytes=64) for a in range(2)]
-            x_codes = [late.tile([P, S], U32, name="x_codes%d" % b, align_bytes=64) for b in range(2)]
-            x_scales = [late.tile([P, S], U8, name="x_scales%d" % b, align_bytes=64) for b in range(2)]
+            x_codes = [late.tile([P, S], U32, name="x_codes%d" % a, align_bytes=64) for a in range(2)]
+            x_scales = [late.tile([P, S], U8, name="x_scales%d" % a, align_bytes=64) for a in range(2)]
             y_codes = [late.tile([P, S], U32, name="y_codes%d" % g, align_bytes=64) for g in range(2)]
-            y_scales = late.tile([P, S], U8, name="y_scales", align_bytes=64)
+            y_scales = [late.tile([P, S], U8, name="y_scales%d" % g, align_bytes=64) for g in range(2)]
             for a in range(2):
                 nc.sync.dma_start(
                     out=w2_raw[a][:].bitcast(I32), in_=w2_words[a].rearrange("p c i -> p (c i)").bitcast(I32)
@@ -338,61 +335,76 @@ def tile_list_blade_tip_page_kernel(
                     in_=w2_scales[:, 4 * q : 4 * q + 4, :].bitcast(I32),
                 )
             nc.vector.tensor_copy(
-                out=w2_scale_dealt[:].rearrange("p (g t m) -> p g m t", g=2, t=4),
-                in_=w2_scale_raw[:].rearrange("p (g m t) -> p g m t", g=2, t=4),
+                out=w2_scale_dealt[:].rearrange("p (g t m) -> p g t m", g=2, t=4),
+                in_=w2_scale_raw[:].rearrange("p (g m t) -> p g t m", g=2, t=4),
             )
 
-            for b in range(2):
-                place_pair(CHUNKS - 1, 2 * b)
-                place_pair(CHUNKS - 1, 2 * b + 1)
-                nc.vector.tensor_copy(
-                    out=w2_dealt[b][:].rearrange("p (g t m) -> p g m t", g=2, t=4),
-                    in_=w2_raw[b][:].rearrange("p (g m t) -> p g m t", g=2, t=4),
-                )
-                for u in range(2):
-                    cols = slice(u * HALF, (u + 1) * HALF)
-                    planes = late.tile([P, 4, HALF], BF16, name="x_planes", tag="x_planes", bufs=2)
-                    for t in range(4):
-                        picked = late.tile([P, HALF], F32, name="picked3", tag="picked3", bufs=4)
-                        nc.vector.tensor_copy(
-                            picked[:], pages[4 * b + t][:].indirect(list3[:, u * HALF // 16 : (u + 1) * HALF // 16])
-                        )
-                        nc.scalar.activation(out=planes[:, t, :], in_=picked[:], func=ACT.Copy, scale=gx_sb[:, b, t : t + 1])
-                    grouped = late.tile([P, 4 * HALF], BF16, name="x_grouped", tag="x_grouped", bufs=2, align_bytes=64)
-                    interleave(nc.scalar.copy, grouped[:], planes[:])
-                    nc.vector.quantize_mx(out=x_codes[b][:, cols].bitcast(FP8X4), scales=x_scales[b][:, cols], in_=grouped[:])
+            def pick(i, places, start, width, name, bufs):
+                picked = late.tile([P, width], F32, name=name, tag=name, bufs=bufs)
+                nc.vector.tensor_copy(picked[:], pages[i][:].indirect(entries(places, start, width)))
+                return picked
+
+            def reread(a, start):
+                cols = slice(start, start + HALF)
+                tiles = late.tile([P, 4, HALF], BF16, name="x_tiles", tag="x_tiles", bufs=2)
+                for t in range(4):
+                    picked = pick(4 * a + t, list3, start, HALF, "reread", 4)
+                    nc.scalar.activation(out=tiles[:, t, :], in_=picked[:], func=ACT.Copy, scale=gx_sb[:, a, t : t + 1])
+                grouped = late.tile([P, 4 * HALF], BF16, name="x_grouped", tag="x_grouped", bufs=2, align_bytes=64)
+                interleave(nc.scalar.copy, grouped[:], tiles[:])
+                nc.vector.quantize_mx(out=x_codes[a][:, cols].bitcast(FP8X4), scales=x_scales[a][:, cols], in_=grouped[:])
 
             y_rows = out_0.rearrange("(g p t) j -> g p t j", g=2, t=4)
-            units = [(0, 0, HALF), (1, 0, HALF), (0, HALF, HALF), (1, HALF, CHUNK), (1, HALF + CHUNK, CHUNK)]
-            for n, (g, start, width) in enumerate(units):
+
+            def finish(g, start, width, copy):
                 cols = slice(start, start + width)
                 y = late.tile([P, 4, width], F32, name="y", tag="y", bufs=2)
                 for t in range(4):
                     i = 4 * g + t
-                    picked = late.tile([P, width], F32, name="picked4", tag="picked4", bufs=6)
-                    nc.vector.tensor_copy(picked[:], pages[i][:].indirect(list4[:, start // 16 : (start + width) // 16]))
+                    near = pick(i, list4, start, width, "near", 6)
                     bank = psum.tile([P, width], F32, name="enc_bank", tag="ph_bank", bufs=3)
-                    for b in range(2):
+                    for a in range(2):
                         nc.tensor.matmul_mx(
                             out=bank[:],
-                            lhsT=w2_dealt[b][:, P * i : P * (i + 1)].bitcast(FP8X4),
-                            lhsT_scale=w2_scale_dealt[4 * b : P, P * i : P * (i + 1)],
-                            rhs=x_codes[b][:, cols].bitcast(FP8X4),
-                            rhs_scale=x_scales[b][:, cols],
-                            start=(b == 0), stop=(b == 1),
+                            lhsT=w2_dealt[a][:, P * i : P * (i + 1)].bitcast(FP8X4),
+                            lhsT_scale=w2_scale_dealt[4 * a : P, P * i : P * (i + 1)],
+                            rhs=x_codes[a][:, cols].bitcast(FP8X4),
+                            rhs_scale=x_scales[a][:, cols],
+                            start=(a == 0), stop=(a == 1),
                         )
                     nc.vector.scalar_tensor_tensor(
-                        out=y[:, t, :], in0=picked[:], scalar=gn_sb[:, g, t : t + 1], in1=bank[:], op0=ALU.mult, op1=ALU.add
+                        out=y[:, t, :], in0=near[:], scalar=gn_sb[:, g, t : t + 1], in1=bank[:], op0=ALU.mult, op1=ALU.add
                     )
                 nc.sync.dma_start(out=y_rows[g][:, :, cols], in_=y[:])
                 grouped = late.tile([P, 4 * width], BF16, name="y_grouped", tag="y_grouped", bufs=2, align_bytes=64)
-                interleave(nc.vector.tensor_copy if n == len(units) - 1 else nc.scalar.copy, grouped[:], y[:])
-                nc.vector.quantize_mx(out=y_codes[g][:, cols].bitcast(FP8X4), scales=y_scales[4 * g : P, cols], in_=grouped[:])
+                interleave(copy, grouped[:], y[:])
+                nc.vector.quantize_mx(out=y_codes[g][:, cols].bitcast(FP8X4), scales=y_scales[g][:, cols], in_=grouped[:])
                 nc.sync.dma_start(
                     out=out_1[g].rearrange("p m t -> p (m t)").bitcast(I32)[:, cols], in_=y_codes[g][:, cols].bitcast(I32)
                 )
-            for q in range(4):
-                queue = nc.scalar if q % 2 == 0 else nc.sync
-                queue.dma_start(
-                    out=out_2[:, 4 * q : 4 * q + 4, :].bitcast(I32), in_=y_scales[32 * q : 32 * q + 8, :].bitcast(I32)
+
+            def store_scales(g):
+                for q in range(4):
+                    queue = nc.scalar if q % 2 == 0 else nc.sync
+                    queue.dma_start(
+                        out=out_2[g, 4 * q : 4 * q + 4, :].bitcast(I32), in_=y_scales[g][32 * q : 32 * q + 4, :].bitcast(I32)
+                    )
+
+            for a in range(2):
+                place_pair(CHUNKS - 1, 2 * a)
+                place_pair(CHUNKS - 1, 2 * a + 1)
+                reread(a, 0)
+            for a in range(2):
+                nc.vector.tensor_copy(
+                    out=w2_dealt[a][:].rearrange("p (g t m) -> p g m t", g=2, t=4),
+                    in_=w2_raw[a][:].rearrange("p (g m t) -> p g m t", g=2, t=4),
                 )
+            for a in range(2):
+                reread(a, HALF)
+            finish(0, 0, HALF, nc.scalar.copy)
+            finish(1, 0, HALF, nc.scalar.copy)
+            finish(0, HALF, HALF, nc.scalar.copy)
+            store_scales(0)
+            finish(1, HALF, HALF // 2, nc.scalar.copy)
+            finish(1, HALF + HALF // 2, HALF // 2, nc.vector.tensor_copy)
+            store_scales(1)

import math
from contextlib import ExitStack

import concourse.mybir as mybir

F32 = mybir.dt.float32
BF16 = mybir.dt.bfloat16
I32 = mybir.dt.int32
U32 = mybir.dt.uint32
U16 = mybir.dt.uint16
U8 = mybir.dt.uint8
FP8X4 = mybir.dt.float8_e4m3fn_x4
FP4X4 = mybir.dt.float4_e2m1fn_x4
ALU = mybir.AluOpType
ACT = mybir.ActivationFunctionType

P = 128
K, T, S, R, H, T2 = 1024, 4096, 1024, 512, 1024, 2048
FLOPS = 2 * (K * R * S + 2 * R * H * S + H * H * S)

GROUP = 512
CHUNK = 256
CHUNKS = S // CHUNK
HALF = S // 2
TWO_PI = 2.0 * math.pi
ROUNDER = 1.5 * 2.0**23


def entries(places, start, count):
    return places[:, start // 16 : (start + count) // 16]


def deal_and_round(copy, grouped, raw):
    copy(out=grouped[:].rearrange("p (t m j) -> p m t j", t=4, j=4), in_=raw[:].rearrange("p j (m t) -> p m t j", t=4))


def interleave(copy, grouped, tiles):
    copy(
        out=grouped.rearrange("p (c i t) -> p c t i", i=4, t=4),
        in_=tiles.rearrange("p t (c i) -> p c t i", i=4),
    )


def tile_list_blade_tip_page_kernel(
    tc, tab_words, tab_scales, offs, w1, gsc, ws_words, ws_scales, wc, page0, wgs, offs2, offs3, gx,
    w2_words, w2_scales, offs4, gn, out_0, out_1, out_2,
):
    nc = tc.nc

    with ExitStack() as ctx:
        keep = ctx.enter_context(tc.tile_pool(name="keep", bufs=1))
        psum = ctx.enter_context(tc.psum_pool(name="psum", bufs=1))

        list1 = keep.tile([P, S // 16], U16, name="list1")
        list2 = keep.tile([P, S // 16], U16, name="list2")
        list3 = keep.tile([P, S // 16], U16, name="list3")
        list4 = keep.tile([P, S // 16], U16, name="list4")
        gsc_sb = keep.tile([P, 2, 4], F32, name="gsc_sb")
        gx_sb = keep.tile([P, 2, 4], F32, name="gx_sb")
        gn_sb = keep.tile([P, 2, 4], F32, name="gn_sb")
        pages = [keep.tile([P, T2], F32, name="page%d" % i) for i in range(8)]
        f_codes = [keep.tile([P, S], U32, name="f_codes%d" % f, align_bytes=64) for f in range(2)]
        f_scales = [keep.tile([P, S], U8, name="f_scales%d" % f, align_bytes=64) for f in range(2)]
        wc_codes = [keep.tile([P, GROUP], U32, name="wc_codes%d" % g, align_bytes=64) for g in range(2)]
        wc_scales = [keep.tile([P, GROUP], U8, name="wc_scales%d" % g, align_bytes=64) for g in range(2)]
        ws_dealt = keep.tile([P, 2 * H], U8, name="ws_dealt", align_bytes=64)
        ws_scale_dealt = keep.tile([P, H], U8, name="ws_scale_dealt", align_bytes=64)

        warm = keep.tile([P, 2], F32, name="warm")
        nc.gpsimd.memset(warm[:, 0:1], 0.0)
        nc.scalar.activation(out=warm[:, 1:2], in_=warm[:, 0:1], func=ACT.Sin)

        page_rows = page0.rearrange("(g p t) c -> g t p c", g=2, t=4)
        wgs_rows = wgs.rearrange("(q t) j -> q t j", t=4)
        wc_rows = wc.rearrange("(p j) c -> p j c", j=4)

        wgs_sb = {}
        hs_sb = {}
        shared = keep.tile([P, 2 * CHUNK], F32, name="shared", align_bytes=64)

        def load_page(i):
            nc.sync.dma_start(out=pages[i][:], in_=page_rows[i // 4, i % 4])

        def load_wgs(c):
            wgs_sb[c] = keep.tile([P, 4, CHUNK], F32, name="wgs_sb", tag="wgs_sb", bufs=2)
            for q in (0, 2, 1, 3):
                nc.sync.dma_start(out=wgs_sb[c][32 * q : 32 * (q + 1)], in_=wgs_rows[:, :, c * CHUNK : (c + 1) * CHUNK])

        def sine_products(c):
            cols = slice(c * CHUNK, (c + 1) * CHUNK)
            for pair in range(4):
                bank = psum.tile([P, 2, CHUNK], F32, name="hs_bank", tag="hs_bank", bufs=2)
                for e in range(2):
                    i = 2 * pair + e
                    nc.tensor.matmul_mx(
                        out=bank[:, e, :],
                        lhsT=ws_dealt[:, 2 * P * i : 2 * P * (i + 1)].bitcast(FP4X4),
                        lhsT_scale=ws_scale_dealt[:, P * i : P * (i + 1)],
                        rhs=f_codes[0][:, cols].bitcast(FP8X4),
                        rhs_scale=f_scales[0][:, cols],
                        start=True, stop=True,
                    )
                hs_sb[c, pair] = keep.tile([P, 2, CHUNK], F32, name="hs_sb", tag="hs_sb", bufs=4)
                nc.scalar.copy(out=hs_sb[c, pair][:], in_=bank[:])

        def place_pair(c, pair):
            cols = slice(c * CHUNK, (c + 1) * CHUNK)
            bank = psum.tile([P, 2, CHUNK], F32, name="hc_bank", tag="hc_bank", bufs=3)
            for e in range(2):
                g, t = divmod(2 * pair + e, 4)
                nc.tensor.matmul_mx(
                    out=bank[:, e, :],
                    lhsT=wc_codes[g][:, P * t : P * (t + 1)].bitcast(FP8X4),
                    lhsT_scale=wc_scales[g][:, P * t : P * (t + 1)],
                    rhs=f_codes[1][:, cols].bitcast(FP8X4),
                    rhs_scale=f_scales[1][:, cols],
                    start=True, stop=True,
                )
            if (c, pair) == (CHUNKS - 2, 3):
                h = shared[:].rearrange("p (e n) -> p e n", e=2)
            else:
                h = keep.tile([P, 2, CHUNK], F32, name="h", tag="h", bufs=2)
            nc.vector.tensor_tensor(out=h[:], in0=bank[:], in1=hs_sb[c, pair][:], op=ALU.max)
            for e in range(2):
                i = 2 * pair + e
                window = pages[i][:].indirect(entries(list2, c * CHUNK, CHUNK))
                nc.vector.tensor_tensor(window, h[:, e, :], wgs_sb[c][:, i % 4, :], ALU.mult)

        with tc.tile_pool(name="early", bufs=1) as early:
            tab_sb = [early.tile([P, T], U32, name="tab_sb%d" % a) for a in range(2)]
            tab_scale_sb = early.tile([P, T], U8, name="tab_scale_sb")
            ws_scale_raw = early.tile([P, H], U8, name="ws_scale_raw")
            ws_raw = early.tile([P, 2 * H], U8, name="ws_raw")
            v_codes = [early.tile([P, S], U32, name="v_codes%d" % a, align_bytes=64) for a in range(2)]
            v_scales = early.tile([P, S], U8, name="v_scales", align_bytes=64)
            w1_codes = [early.tile([P, R], U32, name="w1_codes%d" % a, align_bytes=64) for a in range(2)]
            w1_scales = [early.tile([P, R], U8, name="w1_scales%d" % a, align_bytes=64) for a in range(2)]
            w1_raw = [early.tile([P, 4, R], F32, name="w1_raw%d" % a) for a in range(2)]
            wc_raw0 = early.tile([P, 4, GROUP], F32, name="wc_raw0")

            nc.vector.memset(tab_scale_sb[:].bitcast(I32), 0)
            nc.gpsimd.memset(ws_scale_raw[:].bitcast(I32), 0)

            w1_rows = w1.rearrange("(a p j) c -> a p j c", a=2, j=4)
            nc.sync.dma_start(list1[:], offs)
            nc.sync.dma_start(out=w1_raw[0][:], in_=w1_rows[0])
            for q in range(4):
                nc.sync.dma_start(
                    out=tab_scale_sb[32 * q : 32 * q + 8, :].bitcast(I32),
                    in_=tab_scales[:, 4 * q : 4 * q + 4, :].bitcast(I32),
                )
            nc.sync.dma_start(out=ws_raw[:].bitcast(I32), in_=ws_words[0].bitcast(I32))
            nc.sync.dma_start(out=w1_raw[1][:], in_=w1_rows[1])
            for q in range(4):
                nc.sync.dma_start(
                    out=ws_scale_raw[32 * q : 32 * q + 4, :].bitcast(I32),
                    in_=ws_scales[0, 4 * q : 4 * q + 4, :].bitcast(I32),
                )
            for a in range(2):
                nc.sync.dma_start(
                    out=tab_sb[a][:].bitcast(I32), in_=tab_words[a].rearrange("p t i -> p (t i)").bitcast(I32)
                )
            nc.sync.dma_start(out=wc_raw0[:], in_=wc_rows[:, :, 0:GROUP])
            load_page(0)
            nc.sync.dma_start(out=gsc_sb[:], in_=gsc.rearrange("(f p t) -> p f t", f=2, t=4))
            nc.sync.dma_start(list2[:], offs2)
            load_wgs(0)
            for i in range(1, 4):
                load_page(i)

            w1_grouped = [
                early.tile([P, 4 * R], BF16, name="w1_grouped%d" % a, tag="w_grouped", bufs=2, align_bytes=64)
                for a in range(2)
            ]
            for a in range(2):
                deal_and_round(nc.scalar.copy, w1_grouped[a], w1_raw[a])
            nc.vector.tensor_copy(v_scales[:], tab_scale_sb[:].indirect(list1[:]))
            for a in range(2):
                nc.vector.quantize_mx(out=w1_codes[a][:].bitcast(FP8X4), scales=w1_scales[a][:], in_=w1_grouped[a][:])
            nc.vector.tensor_copy(v_codes[0][:], tab_sb[0][:].indirect(list1[:]))
            nc.vector.tensor_copy(
                out=ws_dealt[:].rearrange("p (g t m e) -> p g t m e", g=2, t=4, e=2),
                in_=ws_raw[:].rearrange("p (g m t e) -> p g t m e", g=2, t=4, e=2),
            )
            nc.vector.tensor_copy(
                out=ws_scale_dealt[:].rearrange("p (g t m) -> p g t m", g=2, t=4),
                in_=ws_scale_raw[:].rearrange("p (g m t) -> p g t m", g=2, t=4),
            )
            for start in (0, HALF):
                nc.vector.tensor_copy(v_codes[1][:, start : start + HALF], tab_sb[1][:].indirect(entries(list1, start, HALF)))

            wc_raw1 = early.tile([P, 4, GROUP], F32, name="wc_raw1")
            nc.sync.dma_start(out=wc_raw1[:], in_=wc_rows[:, :, GROUP : 2 * GROUP])
            for i in range(4, 8):
                load_page(i)
            load_wgs(1)
            nc.sync.dma_start(list3[:], offs3)
            nc.sync.dma_start(list4[:], offs4)
            nc.sync.dma_start(out=gx_sb[:], in_=gx.rearrange("(g p t) -> p g t", g=2, t=4))
            nc.sync.dma_start(out=gn_sb[:], in_=gn.rearrange("(g p t) -> p g t", g=2, t=4))

            def phases(out, t, cols):
                for a in range(2):
                    nc.tensor.matmul_mx(
                        out=out,
                        lhsT=w1_codes[a][:, P * t : P * (t + 1)].bitcast(FP8X4),
                        lhsT_scale=w1_scales[a][:, P * t : P * (t + 1)],
                        rhs=v_codes[a][:, cols].bitcast(FP8X4),
                        rhs_scale=v_scales[4 * a : P, cols],
                        start=(a == 0), stop=(a == 1),
                    )

            def scratch(name, dtype, bufs):
                return early.tile([P, 4 * CHUNK], dtype, name=name, tag=name, bufs=bufs, align_bytes=64)

            def fraction(frac, whole, turns):
                nc.vector.scalar_tensor_tensor(
                    out=frac, in0=whole, scalar=ROUNDER, in1=turns, op0=ALU.subtract, op1=ALU.subtract
                )

            def sine_of(sine, frac):
                nc.scalar.activation(out=sine, in_=frac, func=ACT.Sin, scale=-TWO_PI)

            def cosine_of(cosine, size, frac):
                nc.scalar.activation(out=size, in_=frac, func=ACT.Abs)
                nc.scalar.activation(out=cosine, in_=size, func=ACT.Sin, scale=-TWO_PI, bias=math.pi / 2)

            def quantize_wc(g, copy, raw):
                grouped = early.tile([P, 4 * GROUP], BF16, name="wc_grouped", tag="w_grouped", bufs=2, align_bytes=64)
                deal_and_round(copy, grouped, raw)
                nc.vector.quantize_mx(out=wc_codes[g][:].bitcast(FP8X4), scales=wc_scales[g][:], in_=grouped[:])

            def quantize_features(c, f, grouped):
                cols = slice(c * CHUNK, (c + 1) * CHUNK)
                nc.vector.quantize_mx(out=f_codes[f][:, cols].bitcast(FP8X4), scales=f_scales[f][:, cols], in_=grouped)

            fracs = {}

            def reduce_phases(c):
                turns, whole, fracs[c] = scratch("turns", F32, 1), scratch("whole", I32, 1), scratch("frac", F32, 2)
                for u in range(2):
                    bank = psum.tile([P, 2, CHUNK], F32, name="ph_bank", tag="ph_bank", bufs=3)
                    for e in range(2):
                        phases(bank[:, e, :], 2 * u + e, slice(c * CHUNK, (c + 1) * CHUNK))
                    nc.scalar.activation(
                        out=turns[:, u * 2 * CHUNK : (u + 1) * 2 * CHUNK], in_=bank[:].rearrange("p e n -> p (e n)"),
                        func=ACT.Copy, scale=1.0 / TWO_PI,
                    )
                nc.scalar.activation(out=whole[:].bitcast(U32), in_=turns[:], func=ACT.Copy, bias=ROUNDER)
                fraction(fracs[c][:], whole[:], turns[:])

            def features(c):
                sine, size, cosine = scratch("sine", F32, 1), scratch("size", F32, 1), scratch("cosine", F32, 1)
                sine_of(sine[:], fracs[c][:])
                cosine_of(cosine[:], size[:], fracs[c][:])
                grouped = []
                for f, values in enumerate((sine, cosine)):
                    tiles = early.tile([P, 4, CHUNK], BF16, name="f_tiles%d" % f, tag="f_tiles%d" % f)
                    for t in range(4):
                        nc.scalar.activation(
                            out=tiles[:, t, :], in_=values[:, t * CHUNK : (t + 1) * CHUNK], func=ACT.Copy,
                            scale=gsc_sb[:, f, t : t + 1],
                        )
                    if (c, f) == (CHUNKS - 1, 1):
                        grouped.append(shared[:].bitcast(BF16))
                    else:
                        grouped.append(scratch("f_grouped%d" % f, BF16, 2)[:])
                    interleave(nc.scalar.copy, grouped[f], tiles[:])
                return grouped

            turns, whole, frac = scratch("turns", F32, 1), scratch("whole", I32, 1), scratch("frac", F32, 2)
            sine, size, cosine = scratch("sine", F32, 1), scratch("size", F32, 1), scratch("cosine", F32, 1)
            grouped = [scratch("f_grouped%d" % f, BF16, 2) for f in range(2)]
            parts = [slice(u * 4 * P, (u + 1) * 4 * P) for u in range(CHUNK // P)]
            for u, part in enumerate(parts):
                bank = psum.tile([P, 4, P], F32, name="ph_bank0", tag="ph_bank", bufs=3)
                for t in range(4):
                    phases(bank[:, t, :], t, slice(u * P, (u + 1) * P))
                nc.scalar.activation(
                    out=turns[:, part].rearrange("p (n t) -> p n t", t=4), in_=bank[:].rearrange("p t n -> p n t"),
                    func=ACT.Copy, scale=1.0 / TWO_PI,
                )
                nc.vector.tensor_scalar(out=whole[:, part], in0=turns[:, part], scalar1=ROUNDER, scalar2=None, op0=ALU.add)
                fraction(frac[:, part], whole[:, part], turns[:, part])
                sine_of(sine[:, part], frac[:, part])
            for part in parts:
                cosine_of(cosine[:, part], size[:, part], frac[:, part])
            for f, values in enumerate((sine, cosine)):
                for part in parts:
                    nc.vector.tensor_tensor(
                        out=grouped[f][:, part].rearrange("p (n t) -> p n t", t=4),
                        in0=values[:, part].rearrange("p (n t) -> p n t", t=4),
                        in1=gsc_sb[:, f : f + 1, :].to_broadcast([P, P, 4]),
                        op=ALU.mult,
                    )
                quantize_features(0, f, grouped[f][:])
            quantize_wc(0, nc.vector.tensor_copy, wc_raw0)
            sine_products(0)
            reduce_phases(1)

            for c in range(CHUNKS - 1):
                place_pair(c, 0)
                if c == 0:
                    quantize_wc(1, nc.scalar.copy, wc_raw1)
                grouped = features(c + 1)
                if c + 2 < CHUNKS:
                    reduce_phases(c + 2)
                place_pair(c, 1)
                place_pair(c, 2)
                for f in range(2):
                    quantize_features(c + 1, f, grouped[f])
                sine_products(c + 1)
                place_pair(c, 3)
                if c + 2 < CHUNKS:
                    load_wgs(c + 2)

        with tc.tile_pool(name="late", bufs=1) as late:
            w2_raw = [late.tile([P, H], U32, name="w2_raw%d" % a) for a in range(2)]
            w2_dealt = [late.tile([P, H], U32, name="w2_dealt%d" % a, align_bytes=64) for a in range(2)]
            x_codes = [late.tile([P, S], U32, name="x_codes%d" % a, align_bytes=64) for a in range(2)]
            x_scales = [late.tile([P, S], U8, name="x_scales%d" % a, align_bytes=64) for a in range(2)]
            y_codes = [late.tile([P, S], U32, name="y_codes%d" % g, align_bytes=64) for g in range(2)]
            y_scales = [late.tile([P, S], U8, name="y_scales%d" % g, align_bytes=64) for g in range(2)]
            for a in range(2):
                nc.sync.dma_start(
                    out=w2_raw[a][:].bitcast(I32), in_=w2_words[a].rearrange("p c i -> p (c i)").bitcast(I32)
                )

            w2_scale_raw = late.tile([P, H], U8, name="w2_scale_raw")
            w2_scale_dealt = late.tile([P, H], U8, name="w2_scale_dealt", align_bytes=64)
            nc.gpsimd.memset(w2_scale_raw[:].bitcast(I32), 0)
            for q in range(4):
                nc.sync.dma_start(
                    out=w2_scale_raw[32 * q : 32 * q + 8, :].bitcast(I32),
                    in_=w2_scales[:, 4 * q : 4 * q + 4, :].bitcast(I32),
                )
            nc.vector.tensor_copy(
                out=w2_scale_dealt[:].rearrange("p (g t m) -> p g t m", g=2, t=4),
                in_=w2_scale_raw[:].rearrange("p (g m t) -> p g t m", g=2, t=4),
            )

            def pick(i, places, start, width, name, bufs):
                picked = late.tile([P, width], F32, name=name, tag=name, bufs=bufs)
                nc.vector.tensor_copy(picked[:], pages[i][:].indirect(entries(places, start, width)))
                return picked

            def reread(a, start):
                cols = slice(start, start + HALF)
                tiles = late.tile([P, 4, HALF], BF16, name="x_tiles", tag="x_tiles", bufs=2)
                for t in range(4):
                    picked = pick(4 * a + t, list3, start, HALF, "reread", 4)
                    nc.scalar.activation(out=tiles[:, t, :], in_=picked[:], func=ACT.Copy, scale=gx_sb[:, a, t : t + 1])
                grouped = late.tile([P, 4 * HALF], BF16, name="x_grouped", tag="x_grouped", bufs=2, align_bytes=64)
                interleave(nc.scalar.copy, grouped[:], tiles[:])
                nc.vector.quantize_mx(out=x_codes[a][:, cols].bitcast(FP8X4), scales=x_scales[a][:, cols], in_=grouped[:])

            y_rows = out_0.rearrange("(g p t) j -> g p t j", g=2, t=4)

            def finish(g, start, width, copy):
                cols = slice(start, start + width)
                y = late.tile([P, 4, width], F32, name="y", tag="y", bufs=2)
                for t in range(4):
                    i = 4 * g + t
                    near = pick(i, list4, start, width, "near", 6)
                    bank = psum.tile([P, width], F32, name="enc_bank", tag="ph_bank", bufs=3)
                    for a in range(2):
                        nc.tensor.matmul_mx(
                            out=bank[:],
                            lhsT=w2_dealt[a][:, P * i : P * (i + 1)].bitcast(FP8X4),
                            lhsT_scale=w2_scale_dealt[4 * a : P, P * i : P * (i + 1)],
                            rhs=x_codes[a][:, cols].bitcast(FP8X4),
                            rhs_scale=x_scales[a][:, cols],
                            start=(a == 0), stop=(a == 1),
                        )
                    nc.vector.scalar_tensor_tensor(
                        out=y[:, t, :], in0=near[:], scalar=gn_sb[:, g, t : t + 1], in1=bank[:], op0=ALU.mult, op1=ALU.add
                    )
                nc.sync.dma_start(out=y_rows[g][:, :, cols], in_=y[:])
                grouped = late.tile([P, 4 * width], BF16, name="y_grouped", tag="y_grouped", bufs=2, align_bytes=64)
                interleave(copy, grouped[:], y[:])
                nc.vector.quantize_mx(out=y_codes[g][:, cols].bitcast(FP8X4), scales=y_scales[g][:, cols], in_=grouped[:])
                nc.sync.dma_start(
                    out=out_1[g].rearrange("p m t -> p (m t)").bitcast(I32)[:, cols], in_=y_codes[g][:, cols].bitcast(I32)
                )

            def store_scales(g):
                for q in range(4):
                    queue = nc.scalar if q % 2 == 0 else nc.sync
                    queue.dma_start(
                        out=out_2[g, 4 * q : 4 * q + 4, :].bitcast(I32), in_=y_scales[g][32 * q : 32 * q + 4, :].bitcast(I32)
                    )

            for a in range(2):
                place_pair(CHUNKS - 1, 2 * a)
                place_pair(CHUNKS - 1, 2 * a + 1)
                reread(a, 0)
            for a in range(2):
                nc.vector.tensor_copy(
                    out=w2_dealt[a][:].rearrange("p (g t m) -> p g m t", g=2, t=4),
                    in_=w2_raw[a][:].rearrange("p (g m t) -> p g m t", g=2, t=4),
                )
            for a in range(2):
                reread(a, HALF)
            finish(0, 0, HALF, nc.scalar.copy)
            finish(1, 0, HALF, nc.scalar.copy)
            finish(0, HALF, HALF, nc.scalar.copy)
            store_scales(0)
            finish(1, HALF, HALF // 2, nc.scalar.copy)
            finish(1, HALF + HALF // 2, HALF // 2, nc.vector.tensor_copy)
            store_scales(1)
